import numpy as np
import ml_dtypes


def mxq(x, axis, fmt="e4m3"):
    dtype, down = {"e4m3": (ml_dtypes.float8_e4m3fn, 7), "e5m2": (ml_dtypes.float8_e5m2, 14)}[fmt]
    v = np.moveaxis(np.asarray(x, np.float32).astype(ml_dtypes.bfloat16).astype(np.float64), axis, -1)
    blocks = v.reshape(v.shape[:-1] + (-1, 32))
    amax = np.abs(blocks).max(-1, keepdims=True)
    byte = np.maximum(np.where(amax > 0, np.frexp(amax)[1] - 1 + 127, 0) - down, 1)
    scale = np.exp2(byte - 127.0)
    codes = (blocks / scale).astype(np.float32).astype(dtype).astype(np.float64)
    return np.moveaxis((codes * scale).reshape(v.shape), -1, axis)


WIDE = False


def mx_kscale(k):
    if not WIDE:
        return np.ones(k)
    levels = np.array([10, -10, 5, -5, 0])
    if k % 512:
        return np.exp2(np.random.permutation(np.resize(levels, k // 32))).repeat(32)
    a = np.empty((k // 512, 16))
    for p in range(k // 512):
        a[p, :8] = np.random.permutation(np.resize(levels, 8))
        for g in range(8):
            far = levels[np.abs(levels - a[p, g]) >= 10]
            a[p, g + 8] = far[np.random.randint(len(far))]
    return np.exp2(a.ravel()).repeat(32)


def f64(x):
    return np.asarray(x).astype(np.float64)


def striped(idx):
    return np.tile(idx.reshape(-1, 16).T, (8, 1)).astype(np.uint16)


def unstriped(offs):
    return offs[:16].T.reshape(-1).astype(np.int64)


def striped8(idx):
    return np.concatenate([x.reshape(-1, 16).T for x in idx]).astype(np.uint16)


def runs(offs, k):
    lists = np.stack([offs[16 * r : 16 * r + 16].T.reshape(-1) for r in range(8)]).astype(np.int64)
    return lists[np.arange(k) % 512 // 64]


def pack_weight(w):
    k, n = w.shape
    w = f64(np.asarray(w, np.float32).astype(ml_dtypes.bfloat16)).reshape(k // 32, 32, n)
    amax = np.abs(w).max(1)
    byte = np.clip(np.where(amax > 0, np.frexp(amax)[1] - 1 + 127 - 7, 1), 1, 254)
    scaled = (w * np.exp2(127.0 - byte)[:, None, :]).reshape(k, n).astype(np.float32)
    words = np.ascontiguousarray(scaled.reshape(k // 512, 128, 4, n).transpose(0, 1, 3, 2)).astype(ml_dtypes.float8_e4m3fn).view(np.uint8)
    return words, np.ascontiguousarray(byte.astype(np.uint8).reshape(k // 512, 16, n))


def unpack_weight(words, scales):
    g, p, n, _ = words.shape
    vals = np.ascontiguousarray(words).view(ml_dtypes.float8_e4m3fn).astype(np.float64) * np.repeat(np.exp2(scales.astype(np.float64) - 127.0), 8, axis=1)[..., None]
    return vals.transpose(0, 1, 3, 2).reshape(g * 512, n)

def planes(y):
    n, m = y.shape
    v = y.astype(np.float32).astype(ml_dtypes.bfloat16).astype(np.float64).reshape(n // 32, 32, m)
    top = np.abs(v).max(1)
    byte = np.clip(np.where(top > 0, np.frexp(top)[1] - 1 + 127 - 7, 1), 1, 254)
    codes = (v * np.exp2(127.0 - byte)[:, None, :]).reshape(n, m).astype(np.float32).astype(ml_dtypes.float8_e4m3fn).view(np.uint8)
    words = codes.reshape(n // 512, 128, 4, m).transpose(0, 1, 3, 2)
    return np.ascontiguousarray(words), np.ascontiguousarray(byte.astype(np.uint8).reshape(n // 512, 16, m))


K, T, S, V, N, H = 512, 2048, 512, 256, 512, 512


def setup_inputs():
    n = np.random.standard_normal
    s = mx_kscale(K)[:, None]
    u = mx_kscale(H)
    packed_xT = pack_weight(n((K, T)) * s)
    packed_w2 = pack_weight(n((H, N)) / np.sqrt(H) / u[:, None])
    return {
        "x_words": packed_xT[0],
        "x_scales": packed_xT[1],
        "w1": (n((K, H)) / np.sqrt(K) / s * u).astype(np.float32),
        "w2_words": packed_w2[0],
        "w2_scales": packed_w2[1],
        "offs": striped(np.random.permutation(T)[:S]),
        "s1": striped8(np.stack([np.random.permutation(S)[:V] for _ in range(8)])),
        "d1": striped8(np.stack([np.random.permutation(S)[:V] for _ in range(8)])),
        "s2": striped8(np.stack([np.random.permutation(S)[:V] for _ in range(8)])),
        "d2": striped8(np.stack([np.random.permutation(S)[:V] for _ in range(8)])),
    }


def reference(x_words, x_scales, w1, w2_words, w2_scales, offs, s1, d1, s2, d2):
    xq = unpack_weight(x_words, x_scales)[:, unstriped(offs)]
    y = mxq(f64(w1), 0, "e4m3").T @ xq
    m1 = y[np.arange(H)[:, None], runs(s1, H)]
    h = y.copy()
    h[np.arange(H)[:, None], runs(d1, H)] = m1
    m2 = 0.5 * (h[np.arange(H)[:, None], runs(s2, H)] + h[np.arange(H)[:, None], runs(d2, H)])
    z = h.copy()
    z[np.arange(H)[:, None], runs(d2, H)] = m2
    out_0 = unpack_weight(w2_words, w2_scales).T @ mxq(z, 0, "e4m3")
    return (out_0,) + planes(out_0)

@@ -1,0 +1,189 @@
+from contextlib import ExitStack
+
+import concourse.mybir as mybir
+
+K, T, S, V, N, H = 512, 2048, 512, 256, 512, 512
+FLOPS = 2 * K * H * S + 2 * H * N * S
+
+F32 = mybir.dt.float32
+BF16 = mybir.dt.bfloat16
+I32 = mybir.dt.int32
+U32 = mybir.dt.uint32
+U16 = mybir.dt.uint16
+U8 = mybir.dt.uint8
+FP8X4 = mybir.dt.float8_e4m3fn_x4
+MULT = mybir.AluOpType.mult
+ADD = mybir.AluOpType.add
+
+P = 128
+PACK = 4
+CHUNK = 128
+CHUNKS = S // CHUNK
+HALF = S // 2
+
+
+def load_scale_rows(queue, tile, rows):
+    for q in range(4):
+        queue.dma_start(out=tile[32 * q : 32 * q + 4, :].bitcast(I32), in_=rows[4 * q : 4 * q + 4, :].bitcast(I32))
+
+
+def tile_picked_carry2_none_po_kernel(
+    tc, x_words, x_scales, w1, w2_words, w2_scales, offs, s1, d1, s2, d2, out_0, out_1, out_2
+):
+    nc = tc.nc
+    with ExitStack() as ctx:
+        lists = ctx.enter_context(tc.tile_pool(name="lists", bufs=1))
+        sb = ctx.enter_context(tc.tile_pool(name="sb", bufs=1))
+        psum = ctx.enter_context(tc.psum_pool(name="psum", bufs=1))
+
+        offs_t = lists.tile([P, S // 16], U16, name="offs_t")
+        s1_t = lists.tile([P, V // 16], U16, name="s1_t")
+        d1_t = lists.tile([P, V // 16], U16, name="d1_t")
+        s2_t = lists.tile([P, V // 16], U16, name="s2_t")
+        d2_t = lists.tile([P, V // 16], U16, name="d2_t")
+
+        xs = sb.tile([P, T], U8, name="xs", align_bytes=64)
+        xw = sb.tile([P, T], I32, name="xw", align_bytes=64)
+        w2s = sb.tile([P, N], U8, name="w2s", align_bytes=64)
+        w2w = sb.tile([P, N], I32, name="w2w", align_bytes=64)
+        w1_raw = [sb.tile([P, PACK, H // 2], F32, name="w1_raw%d" % h, align_bytes=64) for h in range(2)]
+
+        nc.vector.memset(xs[:].bitcast(I32), 0)
+        nc.gpsimd.memset(w2s[:].bitcast(I32), 0)
+
+        nc.sync.dma_start(out=offs_t[:], in_=offs)
+        nc.sync.dma_start(out=s1_t[:], in_=s1)
+        nc.sync.dma_start(out=d1_t[:], in_=d1)
+        nc.sync.dma_start(out=s2_t[:], in_=s2)
+        load_scale_rows(nc.scalar, xs, x_scales[0])
+        w1_rows = w1.rearrange("(p j) c -> p j c", j=PACK)
+        for h in range(2):
+            nc.sync.dma_start(out=w1_raw[h][:], in_=w1_rows[:, :, h * (H // 2) : (h + 1) * (H // 2)])
+        nc.sync.dma_start(out=xw[:], in_=x_words[0].rearrange("p c r -> p (c r)").bitcast(I32))
+        load_scale_rows(nc.gpsimd, w2s, w2_scales[0])
+        nc.sync.dma_start(out=d2_t[:], in_=d2)
+        nc.sync.dma_start(out=w2w[:], in_=w2_words[0].rearrange("p c r -> p (c r)").bitcast(I32))
+
+        xsg = sb.tile([P, S], U8, name="xsg", align_bytes=64)
+        nc.vector.tensor_copy(out=xsg[:], in_=xs[:].indirect(offs_t[:]))
+
+        w1g = sb.tile([P, PACK, P, PACK], BF16, name="w1g", align_bytes=64)
+        for h in range(2):
+            dst = w1g[:, :, h * (P // 2) : (h + 1) * (P // 2), :].rearrange("p t m j -> p m j t")
+            src = w1_raw[h][:].rearrange("p j (m t) -> p m j t", t=PACK)
+            if h == 0:
+                nc.scalar.copy(out=dst, in_=src)
+            else:
+                nc.vector.tensor_copy(out=dst, in_=src)
+        w1q = sb.tile([P, H], U32, name="w1q", align_bytes=64)
+        w1s = sb.tile([P, H], U8, name="w1s", align_bytes=64)
+        w1flat = w1g[:].rearrange("p t m j -> p (t m j)")
+        for h in range(2):
+            cols = slice(h * (H // 2), (h + 1) * (H // 2))
+            nc.vector.quantize_mx(
+                out=w1q[:, cols].bitcast(FP8X4),
+                scales=w1s[:, cols],
+                in_=w1flat[:, h * 2 * H : (h + 1) * 2 * H],
+            )
+
+        xg = sb.tile([P, S], U32, name="xg", align_bytes=64)
+        for h in range(2):
+            nc.vector.tensor_copy(
+                out=xg[:, h * HALF : (h + 1) * HALF],
+                in_=xw[:].bitcast(U32).indirect(offs_t[:, h * (HALF // 16) : (h + 1) * (HALF // 16)]),
+            )
+
+        w2d = sb.tile([P, N], I32, name="w2d", align_bytes=64)
+        w2sd = sb.tile([P, N], U8, name="w2sd", align_bytes=64)
+        nc.vector.tensor_copy(
+            out=w2d[:].rearrange("p (t m) -> p m t", t=PACK), in_=w2w[:].rearrange("p (m t) -> p m t", t=PACK)
+        )
+        nc.vector.tensor_copy(
+            out=w2sd[:].rearrange("p (t m) -> p m t", t=PACK), in_=w2s[:].rearrange("p (m t) -> p m t", t=PACK)
+        )
+
+        state = [sb.tile([P, S], F32, name="state%d" % t, align_bytes=64) for t in range(PACK)]
+        for t in range(PACK):
+            m_cols = slice(t * P, (t + 1) * P)
+            pieces = [slice(0, HALF), slice(HALF, S)] if t == 0 else [slice(0, S)]
+            for i, cols in enumerate(pieces):
+                acc = psum.tile([P, cols.stop - cols.start], F32, name="y_acc", tag="bank%d" % (t + i + (t > 0)))
+                nc.tensor.matmul_mx(
+                    out=acc[:],
+                    lhsT=w1q[:, m_cols].bitcast(FP8X4),
+                    lhsT_scale=w1s[:, m_cols],
+                    rhs=xg[:, cols].bitcast(FP8X4),
+                    rhs_scale=xsg[:, cols],
+                    start=True,
+                    stop=True,
+                )
+                nc.scalar.copy(out=state[t][:, cols], in_=acc[:])
+
+        moved = [sb.tile([P, V], F32, name="moved%d" % t) for t in range(PACK)]
+        half_s = [sb.tile([P, V], F32, name="half_s%d" % t) for t in range(PACK)]
+        half_d = [sb.tile([P, V], F32, name="half_d%d" % t) for t in range(PACK)]
+        zb = [sb.tile([P, CHUNK, PACK], BF16, name="zb%d" % c, align_bytes=64) for c in range(CHUNKS)]
+
+        def fetch1(t):
+            nc.vector.tensor_copy(out=moved[t][:], in_=state[t][:].indirect(s1_t[:]))
+
+        def put1(t):
+            nc.vector.tensor_copy(out=state[t][:].indirect(d1_t[:]), in_=moved[t][:])
+
+        def fetch2(t):
+            nc.vector.tensor_scalar(half_s[t][:], state[t][:].indirect(s2_t[:]), 0.5, 0.0, MULT, ADD)
+            nc.vector.tensor_scalar(half_d[t][:], state[t][:].indirect(d2_t[:]), 0.5, 0.0, MULT, ADD)
+
+        def put2(t):
+            nc.vector.tensor_tensor(state[t][:].indirect(d2_t[:]), half_s[t][:], half_d[t][:], ADD)
+            for c in range(CHUNKS):
+                nc.scalar.copy(out=zb[c][:, :, t], in_=state[t][:, c * CHUNK : (c + 1) * CHUNK])
+
+        stages = [fetch1, put1, fetch2, put2]
+        for step in range(PACK + len(stages) - 1):
+            for t in range(PACK):
+                if 0 <= step - t < len(stages):
+                    stages[step - t](t)
+
+        zq = sb.tile([P, S], U32, name="zq", align_bytes=64)
+        zs = sb.tile([P, S], U8, name="zs", align_bytes=64)
+        oq = sb.tile([P, S], U32, name="oq", align_bytes=64)
+        osc = sb.tile([P, S], U8, name="osc", align_bytes=64)
+        out_rows = out_0.rearrange("(p t) j -> p t j", t=PACK)
+        out_words = out_1[0].rearrange("p c r -> p (c r)").bitcast(I32)
+
+        for c in range(CHUNKS):
+            cols = slice(c * CHUNK, (c + 1) * CHUNK)
+            nc.vector.quantize_mx(
+                out=zq[:, cols].bitcast(FP8X4), scales=zs[:, cols], in_=zb[c][:].rearrange("p n t -> p (n t)")
+            )
+        for c in range(CHUNKS):
+            cols = slice(c * CHUNK, (c + 1) * CHUNK)
+            acc = psum.tile([P, PACK, CHUNK], F32, name="o_acc", tag="bank%d" % ((5 + c) % 8))
+            for t in range(PACK):
+                m_cols = slice(t * P, (t + 1) * P)
+                nc.tensor.matmul_mx(
+                    out=acc[:, t, :],
+                    lhsT=w2d[:, m_cols].bitcast(FP8X4),
+                    lhsT_scale=w2sd[:, m_cols],
+                    rhs=zq[:, cols].bitcast(FP8X4),
+                    rhs_scale=zs[:, cols],
+                    start=True,
+                    stop=True,
+                )
+            o32 = sb.tile([P, PACK, CHUNK], F32, name="o32_%d" % c)
+            nc.scalar.copy(out=o32[:], in_=acc[:])
+            nc.sync.dma_start(out=out_rows[:, :, cols], in_=o32[:])
+            ob = sb.tile([P, CHUNK, PACK], BF16, name="ob%d" % c, align_bytes=64)
+            nc.vector.tensor_copy(out=ob[:], in_=o32[:].rearrange("p t n -> p n t"))
+            nc.vector.quantize_mx(
+                out=oq[:, cols].bitcast(FP8X4), scales=osc[:, cols], in_=ob[:].rearrange("p n t -> p (n t)")
+            )
+            if c % 2 == 1:
+                both = slice((c - 1) * CHUNK, (c + 1) * CHUNK)
+                nc.sync.dma_start(out=out_words[:, both], in_=oq[:, both].bitcast(I32))
+        for q in range(4):
+            queue = nc.scalar if q % 2 == 0 else nc.sync
+            queue.dma_start(
+                out=out_2[0, 4 * q : 4 * q + 4, :].bitcast(I32), in_=osc[32 * q : 32 * q + 4, :].bitcast(I32)
+            )

@@ -20,11 +20,12 @@ PACK = 4
 CHUNK = 128
 CHUNKS = S // CHUNK
 HALF = S // 2
+ORDER = (2, 0, 1, 3)
 
 
-def load_scale_rows(queue, tile, rows):
-    for q in range(4):
-        queue.dma_start(out=tile[32 * q : 32 * q + 4, :].bitcast(I32), in_=rows[4 * q : 4 * q + 4, :].bitcast(I32))
+def load_scale_rows(queue, tile, rows, quadrants=range(4)):
+    for q in quadrants:
+        queue.dma_start(out=tile[32 * q : 32 * q + 4, :], in_=rows[4 * q : 4 * q + 4, :].bitcast(I32))
 
 
 def tile_picked_carry2_none_po_kernel(
@@ -34,6 +35,7 @@ def tile_picked_carry2_none_po_kernel(
     with ExitStack() as ctx:
         lists = ctx.enter_context(tc.tile_pool(name="lists", bufs=1))
         sb = ctx.enter_context(tc.tile_pool(name="sb", bufs=1))
+        shared = ctx.enter_context(tc.tile_pool(name="shared", bufs=1))
         psum = ctx.enter_context(tc.psum_pool(name="psum", bufs=1))
 
         offs_t = lists.tile([P, S // 16], U16, name="offs_t")
@@ -43,7 +45,8 @@ def tile_picked_carry2_none_po_kernel(
         d2_t = lists.tile([P, V // 16], U16, name="d2_t")
 
         xs = sb.tile([P, T], U8, name="xs", align_bytes=64)
-        xw = sb.tile([P, T], I32, name="xw", align_bytes=64)
+        xs_rows = sb.tile([P, T // 4], I32, name="xs_rows", align_bytes=64)
+        xw = shared.tile([P, T], I32, name="xw", align_bytes=64, offset=0)
         w2s = sb.tile([P, N], U8, name="w2s", align_bytes=64)
         w2w = sb.tile([P, N], I32, name="w2w", align_bytes=64)
         w1_raw = [sb.tile([P, PACK, H // 2], F32, name="w1_raw%d" % h, align_bytes=64) for h in range(2)]
@@ -51,19 +54,23 @@ def tile_picked_carry2_none_po_kernel(
         nc.vector.memset(xs[:].bitcast(I32), 0)
         nc.gpsimd.memset(w2s[:].bitcast(I32), 0)
 
+        load_scale_rows(nc.sync, xs_rows, x_scales[0], (0, 1))
+        load_scale_rows(nc.scalar, xs_rows, x_scales[0], (2, 3))
+        w1_rows = w1.rearrange("(p j) c -> p j c", j=PACK)
+        nc.sync.dma_start(out=w1_raw[0][:], in_=w1_rows[:, :, : H // 2])
         nc.sync.dma_start(out=offs_t[:], in_=offs)
+        nc.sync.dma_start(out=w1_raw[1][:], in_=w1_rows[:, :, H // 2 :])
+        nc.sync.dma_start(out=xw[:], in_=x_words[0].rearrange("p c r -> p (c r)").bitcast(I32))
+        load_scale_rows(nc.gpsimd, w2s[:].bitcast(I32), w2_scales[0])
         nc.sync.dma_start(out=s1_t[:], in_=s1)
+        nc.sync.dma_start(out=w2w[:], in_=w2_words[0].rearrange("p c r -> p (c r)").bitcast(I32))
         nc.sync.dma_start(out=d1_t[:], in_=d1)
         nc.sync.dma_start(out=s2_t[:], in_=s2)
-        load_scale_rows(nc.scalar, xs, x_scales[0])
-        w1_rows = w1.rearrange("(p j) c -> p j c", j=PACK)
-        for h in range(2):
-            nc.sync.dma_start(out=w1_raw[h][:], in_=w1_rows[:, :, h * (H // 2) : (h + 1) * (H // 2)])
-        nc.sync.dma_start(out=xw[:], in_=x_words[0].rearrange("p c r -> p (c r)").bitcast(I32))
-        load_scale_rows(nc.gpsimd, w2s, w2_scales[0])
         nc.sync.dma_start(out=d2_t[:], in_=d2)
-        nc.sync.dma_start(out=w2w[:], in_=w2_words[0].rearrange("p c r -> p (c r)").bitcast(I32))
 
+        for q in range(4):
+            rows = slice(32 * q, 32 * q + 4)
+            nc.vector.tensor_copy(out=xs[rows, :].bitcast(I32), in_=xs_rows[rows, :])
         xsg = sb.tile([P, S], U8, name="xsg", align_bytes=64)
         nc.vector.tensor_copy(out=xsg[:], in_=xs[:].indirect(offs_t[:]))
 
@@ -78,7 +85,7 @@ def tile_picked_carry2_none_po_kernel(
         w1q = sb.tile([P, H], U32, name="w1q", align_bytes=64)
         w1s = sb.tile([P, H], U8, name="w1s", align_bytes=64)
         w1flat = w1g[:].rearrange("p t m j -> p (t m j)")
-        for h in range(2):
+        for h in (1, 0):
             cols = slice(h * (H // 2), (h + 1) * (H // 2))
             nc.vector.quantize_mx(
                 out=w1q[:, cols].bitcast(FP8X4),
@@ -93,8 +100,8 @@ def tile_picked_carry2_none_po_kernel(
                 in_=xw[:].bitcast(U32).indirect(offs_t[:, h * (HALF // 16) : (h + 1) * (HALF // 16)]),
             )
 
-        w2d = sb.tile([P, N], I32, name="w2d", align_bytes=64)
-        w2sd = sb.tile([P, N], U8, name="w2sd", align_bytes=64)
+        w2d = shared.tile([P, N], I32, name="w2d", align_bytes=64, offset=0)
+        w2sd = shared.tile([P, N], U8, name="w2sd", align_bytes=64, offset=4 * N)
         nc.vector.tensor_copy(
             out=w2d[:].rearrange("p (t m) -> p m t", t=PACK), in_=w2w[:].rearrange("p (m t) -> p m t", t=PACK)
         )
@@ -103,11 +110,11 @@ def tile_picked_carry2_none_po_kernel(
         )
 
         state = [sb.tile([P, S], F32, name="state%d" % t, align_bytes=64) for t in range(PACK)]
-        for t in range(PACK):
+        for n, t in enumerate(ORDER):
             m_cols = slice(t * P, (t + 1) * P)
-            pieces = [slice(0, HALF), slice(HALF, S)] if t == 0 else [slice(0, S)]
+            pieces = [slice(0, HALF), slice(HALF, S)] if n == 0 else [slice(0, S)]
             for i, cols in enumerate(pieces):
-                acc = psum.tile([P, cols.stop - cols.start], F32, name="y_acc", tag="bank%d" % (t + i + (t > 0)))
+                acc = psum.tile([P, cols.stop - cols.start], F32, name="y_acc", tag="bank%d" % (n + i + (n > 0)))
                 nc.tensor.matmul_mx(
                     out=acc[:],
                     lhsT=w1q[:, m_cols].bitcast(FP8X4),
@@ -120,7 +127,7 @@ def tile_picked_carry2_none_po_kernel(
                 nc.scalar.copy(out=state[t][:, cols], in_=acc[:])
 
         moved = [sb.tile([P, V], F32, name="moved%d" % t) for t in range(PACK)]
-        half_s = [sb.tile([P, V], F32, name="half_s%d" % t) for t in range(PACK)]
+        half_s = {}
         half_d = [sb.tile([P, V], F32, name="half_d%d" % t) for t in range(PACK)]
         zb = [sb.tile([P, CHUNK, PACK], BF16, name="zb%d" % c, align_bytes=64) for c in range(CHUNKS)]
 
@@ -131,19 +138,26 @@ def tile_picked_carry2_none_po_kernel(
             nc.vector.tensor_copy(out=state[t][:].indirect(d1_t[:]), in_=moved[t][:])
 
         def fetch2(t):
+            if t == ORDER[-1]:
+                half_s[t] = sb.tile([P, V], F32, name="half_s_last", tag="state%d" % ORDER[0], align_bytes=64)
+            else:
+                half_s[t] = sb.tile([P, V], F32, name="half_s%d" % t)
             nc.vector.tensor_scalar(half_s[t][:], state[t][:].indirect(s2_t[:]), 0.5, 0.0, MULT, ADD)
             nc.vector.tensor_scalar(half_d[t][:], state[t][:].indirect(d2_t[:]), 0.5, 0.0, MULT, ADD)
 
         def put2(t):
             nc.vector.tensor_tensor(state[t][:].indirect(d2_t[:]), half_s[t][:], half_d[t][:], ADD)
             for c in range(CHUNKS):
-                nc.scalar.copy(out=zb[c][:, :, t], in_=state[t][:, c * CHUNK : (c + 1) * CHUNK])
+                if t == ORDER[-1] and c < 2:
+                    nc.vector.tensor_copy(out=zb[c][:, :, t], in_=state[t][:, c * CHUNK : (c + 1) * CHUNK])
+                else:
+                    nc.scalar.copy(out=zb[c][:, :, t], in_=state[t][:, c * CHUNK : (c + 1) * CHUNK])
 
         stages = [fetch1, put1, fetch2, put2]
         for step in range(PACK + len(stages) - 1):
-            for t in range(PACK):
-                if 0 <= step - t < len(stages):
-                    stages[step - t](t)
+            for n in reversed(range(PACK)):
+                if 0 <= step - n < len(stages):
+                    stages[step - n](ORDER[n])
 
         zq = sb.tile([P, S], U32, name="zq", align_bytes=64)
         zs = sb.tile([P, S], U8, name="zs", align_bytes=64)
@@ -159,20 +173,22 @@ def tile_picked_carry2_none_po_kernel(
             )
         for c in range(CHUNKS):
             cols = slice(c * CHUNK, (c + 1) * CHUNK)
-            acc = psum.tile([P, PACK, CHUNK], F32, name="o_acc", tag="bank%d" % ((5 + c) % 8))
-            for t in range(PACK):
-                m_cols = slice(t * P, (t + 1) * P)
-                nc.tensor.matmul_mx(
-                    out=acc[:, t, :],
-                    lhsT=w2d[:, m_cols].bitcast(FP8X4),
-                    lhsT_scale=w2sd[:, m_cols],
-                    rhs=zq[:, cols].bitcast(FP8X4),
-                    rhs_scale=zs[:, cols],
-                    start=True,
-                    stop=True,
-                )
             o32 = sb.tile([P, PACK, CHUNK], F32, name="o32_%d" % c)
-            nc.scalar.copy(out=o32[:], in_=acc[:])
+            groups = [range(0, 2), range(2, 4)] if c == CHUNKS - 1 else [range(PACK)]
+            for i, group in enumerate(groups):
+                acc = psum.tile([P, len(group), CHUNK], F32, name="o_acc", tag="bank%d" % ((5 + c + i) % 8))
+                for t in group:
+                    m_cols = slice(t * P, (t + 1) * P)
+                    nc.tensor.matmul_mx(
+                        out=acc[:, t - group.start, :],
+                        lhsT=w2d[:, m_cols].bitcast(FP8X4),
+                        lhsT_scale=w2sd[:, m_cols],
+                        rhs=zq[:, cols].bitcast(FP8X4),
+                        rhs_scale=zs[:, cols],
+                        start=True,
+                        stop=True,
+                    )
+                nc.scalar.copy(out=o32[:, group.start : group.stop, :], in_=acc[:])
             nc.sync.dma_start(out=out_rows[:, :, cols], in_=o32[:])
             ob = sb.tile([P, CHUNK, PACK], BF16, name="ob%d" % c, align_bytes=64)
             nc.vector.tensor_copy(out=ob[:], in_=o32[:].rearrange("p t n -> p n t"))
@@ -181,7 +197,7 @@ def tile_picked_carry2_none_po_kernel(
             )
             if c % 2 == 1:
                 both = slice((c - 1) * CHUNK, (c + 1) * CHUNK)
-                nc.sync.dma_start(out=out_words[:, both], in_=oq[:, both].bitcast(I32))
+                nc.scalar.dma_start(out=out_words[:, both], in_=oq[:, both].bitcast(I32))
         for q in range(4):
             queue = nc.scalar if q % 2 == 0 else nc.sync
             queue.dma_start(

@@ -17,8 +17,7 @@ ADD = mybir.AluOpType.add
 
 P = 128
 PACK = 4
-CHUNK = 128
-CHUNKS = S // CHUNK
+CHUNKS = (slice(0, 128), slice(128, 384), slice(384, 512))
 HALF = S // 2
 ORDER = (2, 0, 1, 3)
 
@@ -82,16 +81,22 @@ def tile_picked_carry2_none_po_kernel(
                 nc.scalar.copy(out=dst, in_=src)
             else:
                 nc.vector.tensor_copy(out=dst, in_=src)
-        w1q = sb.tile([P, H], U32, name="w1q", align_bytes=64)
-        w1s = sb.tile([P, H], U8, name="w1s", align_bytes=64)
+        w1q = {
+            1: sb.tile([P, H // 2], U32, name="w1q1", align_bytes=64),
+            0: shared.tile([P, H // 2], U32, name="w1q0", align_bytes=64, offset=5 * N),
+        }
+        w1s = {
+            1: sb.tile([P, H // 2], U8, name="w1s1", align_bytes=64),
+            0: shared.tile([P, H // 2], U8, name="w1s0", align_bytes=64, offset=7 * N),
+        }
         w1flat = w1g[:].rearrange("p t m j -> p (t m j)")
-        for h in (1, 0):
-            cols = slice(h * (H // 2), (h + 1) * (H // 2))
+
+        def quantise_w1(h):
             nc.vector.quantize_mx(
-                out=w1q[:, cols].bitcast(FP8X4),
-                scales=w1s[:, cols],
-                in_=w1flat[:, h * 2 * H : (h + 1) * 2 * H],
+                out=w1q[h][:].bitcast(FP8X4), scales=w1s[h][:], in_=w1flat[:, h * 2 * H : (h + 1) * 2 * H]
             )
+
+        quantise_w1(1)
 
         xg = sb.tile([P, S], U32, name="xg", align_bytes=64)
         for h in range(2):
@@ -99,6 +104,8 @@ def tile_picked_carry2_none_po_kernel(
                 out=xg[:, h * HALF : (h + 1) * HALF],
                 in_=xw[:].bitcast(U32).indirect(offs_t[:, h * (HALF // 16) : (h + 1) * (HALF // 16)]),
             )
+
+        quantise_w1(0)
 
         w2d = shared.tile([P, N], I32, name="w2d", align_bytes=64, offset=0)
         w2sd = shared.tile([P, N], U8, name="w2sd", align_bytes=64, offset=4 * N)
@@ -111,14 +118,14 @@ def tile_picked_carry2_none_po_kernel(
 
         state = [sb.tile([P, S], F32, name="state%d" % t, align_bytes=64) for t in range(PACK)]
         for n, t in enumerate(ORDER):
-            m_cols = slice(t * P, (t + 1) * P)
+            m_cols = slice(t % 2 * P, (t % 2 + 1) * P)
             pieces = [slice(0, HALF), slice(HALF, S)] if n == 0 else [slice(0, S)]
             for i, cols in enumerate(pieces):
                 acc = psum.tile([P, cols.stop - cols.start], F32, name="y_acc", tag="bank%d" % (n + i + (n > 0)))
                 nc.tensor.matmul_mx(
                     out=acc[:],
-                    lhsT=w1q[:, m_cols].bitcast(FP8X4),
-                    lhsT_scale=w1s[:, m_cols],
+                    lhsT=w1q[t // 2][:, m_cols].bitcast(FP8X4),
+                    lhsT_scale=w1s[t // 2][:, m_cols],
                     rhs=xg[:, cols].bitcast(FP8X4),
                     rhs_scale=xsg[:, cols],
                     start=True,
@@ -129,7 +136,10 @@ def tile_picked_carry2_none_po_kernel(
         moved = [sb.tile([P, V], F32, name="moved%d" % t) for t in range(PACK)]
         half_s = {}
         half_d = [sb.tile([P, V], F32, name="half_d%d" % t) for t in range(PACK)]
-        zb = [sb.tile([P, CHUNK, PACK], BF16, name="zb%d" % c, align_bytes=64) for c in range(CHUNKS)]
+        zb = [
+            sb.tile([P, cols.stop - cols.start, PACK], BF16, name="zb%d" % c, align_bytes=64)
+            for c, cols in enumerate(CHUNKS)
+        ]
 
         def fetch1(t):
             nc.vector.tensor_copy(out=moved[t][:], in_=state[t][:].indirect(s1_t[:]))
@@ -147,11 +157,14 @@ def tile_picked_carry2_none_po_kernel(
 
         def put2(t):
             nc.vector.tensor_tensor(state[t][:].indirect(d2_t[:]), half_s[t][:], half_d[t][:], ADD)
-            for c in range(CHUNKS):
-                if t == ORDER[-1] and c < 2:
-                    nc.vector.tensor_copy(out=zb[c][:, :, t], in_=state[t][:, c * CHUNK : (c + 1) * CHUNK])
-                else:
-                    nc.scalar.copy(out=zb[c][:, :, t], in_=state[t][:, c * CHUNK : (c + 1) * CHUNK])
+            for c, cols in enumerate(CHUNKS):
+                if t != ORDER[-1]:
+                    nc.scalar.copy(out=zb[c][:, :, t], in_=state[t][:, cols])
+            if t == ORDER[-1]:
+                nc.vector.tensor_copy(out=zb[0][:, :, t], in_=state[t][:, 0:128])
+                nc.vector.tensor_copy(out=zb[1][:, 0:128, t], in_=state[t][:, 128:256])
+                nc.scalar.copy(out=zb[1][:, 128:256, t], in_=state[t][:, 256:384])
+                nc.scalar.copy(out=zb[2][:, :, t], in_=state[t][:, 384:512])
 
         stages = [fetch1, put1, fetch2, put2]
         for step in range(PACK + len(stages) - 1):
@@ -166,21 +179,20 @@ def tile_picked_carry2_none_po_kernel(
         out_rows = out_0.rearrange("(p t) j -> p t j", t=PACK)
         out_words = out_1[0].rearrange("p c r -> p (c r)").bitcast(I32)
 
-        for c in range(CHUNKS):
-            cols = slice(c * CHUNK, (c + 1) * CHUNK)
+        for c, cols in enumerate(CHUNKS):
             nc.vector.quantize_mx(
                 out=zq[:, cols].bitcast(FP8X4), scales=zs[:, cols], in_=zb[c][:].rearrange("p n t -> p (n t)")
             )
-        for c in range(CHUNKS):
-            cols = slice(c * CHUNK, (c + 1) * CHUNK)
-            o32 = sb.tile([P, PACK, CHUNK], F32, name="o32_%d" % c)
-            groups = [range(0, 2), range(2, 4)] if c == CHUNKS - 1 else [range(PACK)]
-            for i, group in enumerate(groups):
-                acc = psum.tile([P, len(group), CHUNK], F32, name="o_acc", tag="bank%d" % ((5 + c + i) % 8))
-                for t in group:
+        for c, cols in enumerate(CHUNKS):
+            width = cols.stop - cols.start
+            o32 = sb.tile([P, PACK, width], F32, name="o32_%d" % c)
+            for i in range(2):
+                pair = slice(2 * i, 2 * i + 2)
+                acc = psum.tile([P, 2, width], F32, name="o_acc", tag="bank%d" % ((5 + 2 * c + i) % 8))
+                for t in range(pair.start, pair.stop):
                     m_cols = slice(t * P, (t + 1) * P)
                     nc.tensor.matmul_mx(
-                        out=acc[:, t - group.start, :],
+                        out=acc[:, t - pair.start, :],
                         lhsT=w2d[:, m_cols].bitcast(FP8X4),
                         lhsT_scale=w2sd[:, m_cols],
                         rhs=zq[:, cols].bitcast(FP8X4),
@@ -188,16 +200,21 @@ def tile_picked_carry2_none_po_kernel(
                         start=True,
                         stop=True,
                     )
-                nc.scalar.copy(out=o32[:, group.start : group.stop, :], in_=acc[:])
-            nc.sync.dma_start(out=out_rows[:, :, cols], in_=o32[:])
-            ob = sb.tile([P, CHUNK, PACK], BF16, name="ob%d" % c, align_bytes=64)
-            nc.vector.tensor_copy(out=ob[:], in_=o32[:].rearrange("p t n -> p n t"))
+                nc.scalar.copy(out=o32[:, pair, :], in_=acc[:])
+                if c < len(CHUNKS) - 1:
+                    nc.sync.dma_start(out=out_rows[:, pair, cols], in_=o32[:, pair, :])
+            if c == len(CHUNKS) - 1:
+                nc.sync.dma_start(out=out_rows[:, :, cols], in_=o32[:])
+            ob = sb.tile([P, width, PACK], BF16, name="ob%d" % c, align_bytes=64)
+            nc.vector.tensor_copy(
+                out=ob[:].rearrange("p (n i) t -> p n t i", i=4), in_=o32[:].rearrange("p t (n i) -> p n t i", i=4)
+            )
             nc.vector.quantize_mx(
                 out=oq[:, cols].bitcast(FP8X4), scales=osc[:, cols], in_=ob[:].rearrange("p n t -> p (n t)")
             )
-            if c % 2 == 1:
-                both = slice((c - 1) * CHUNK, (c + 1) * CHUNK)
-                nc.scalar.dma_start(out=out_words[:, both], in_=oq[:, both].bitcast(I32))
+            if c > 0:
+                done = slice(0, cols.stop) if c == 1 else cols
+                nc.scalar.dma_start(out=out_words[:, done], in_=oq[:, done].bitcast(I32))
         for q in range(4):
             queue = nc.scalar if q % 2 == 0 else nc.sync
             queue.dma_start(

@@ -19,7 +19,8 @@ P = 128
 PACK = 4
 CHUNKS = (slice(0, 128), slice(128, 384), slice(384, 512))
 HALF = S // 2
-ORDER = (2, 0, 1, 3)
+ORDER = (0, 2, 3, 1)
+SPLIT = 48
 
 
 def load_scale_rows(queue, tile, rows, quadrants=range(4)):
@@ -43,60 +44,51 @@ def tile_picked_carry2_none_po_kernel(
         s2_t = lists.tile([P, V // 16], U16, name="s2_t")
         d2_t = lists.tile([P, V // 16], U16, name="d2_t")
 
-        xs = sb.tile([P, T], U8, name="xs", align_bytes=64)
+        xs = shared.tile([P, T], U8, name="xs", align_bytes=64, offset=4 * T)
         xs_rows = sb.tile([P, T // 4], I32, name="xs_rows", align_bytes=64)
         xw = shared.tile([P, T], I32, name="xw", align_bytes=64, offset=0)
+        xsm = sb.tile([P, S], U8, name="xsm", align_bytes=64)
         w2s = sb.tile([P, N], U8, name="w2s", align_bytes=64)
-        w2w = sb.tile([P, N], I32, name="w2w", align_bytes=64)
-        w1_raw = [sb.tile([P, PACK, H // 2], F32, name="w1_raw%d" % h, align_bytes=64) for h in range(2)]
+        w1_raw = sb.tile([P, PACK, H], F32, name="w1_raw", align_bytes=64)
 
         nc.vector.memset(xs[:].bitcast(I32), 0)
+        nc.gpsimd.memset(xsm[:].bitcast(I32), 0)
         nc.gpsimd.memset(w2s[:].bitcast(I32), 0)
 
-        load_scale_rows(nc.sync, xs_rows, x_scales[0], (0, 1))
-        load_scale_rows(nc.scalar, xs_rows, x_scales[0], (2, 3))
-        w1_rows = w1.rearrange("(p j) c -> p j c", j=PACK)
-        nc.sync.dma_start(out=w1_raw[0][:], in_=w1_rows[:, :, : H // 2])
+        nc.sync.dma_start(out=xs_rows[0:16, :], in_=x_scales[0].bitcast(I32))
         nc.sync.dma_start(out=offs_t[:], in_=offs)
-        nc.sync.dma_start(out=w1_raw[1][:], in_=w1_rows[:, :, H // 2 :])
-        nc.sync.dma_start(out=xw[:], in_=x_words[0].rearrange("p c r -> p (c r)").bitcast(I32))
-        load_scale_rows(nc.gpsimd, w2s[:].bitcast(I32), w2_scales[0])
+        nc.sync.dma_start(out=w1_raw[:], in_=w1.rearrange("(p j) c -> p j c", j=PACK))
         nc.sync.dma_start(out=s1_t[:], in_=s1)
-        nc.sync.dma_start(out=w2w[:], in_=w2_words[0].rearrange("p c r -> p (c r)").bitcast(I32))
         nc.sync.dma_start(out=d1_t[:], in_=d1)
+        nc.sync.dma_start(out=xw[:], in_=x_words[0].rearrange("p c r -> p (c r)").bitcast(I32))
         nc.sync.dma_start(out=s2_t[:], in_=s2)
         nc.sync.dma_start(out=d2_t[:], in_=d2)
+        load_scale_rows(nc.gpsimd, w2s[:].bitcast(I32), w2_scales[0])
 
-        for q in range(4):
-            rows = slice(32 * q, 32 * q + 4)
-            nc.vector.tensor_copy(out=xs[rows, :].bitcast(I32), in_=xs_rows[rows, :])
+        nc.vector.tensor_copy(out=xs[0:16, :].bitcast(I32), in_=xs_rows[0:16, :])
         xsg = sb.tile([P, S], U8, name="xsg", align_bytes=64)
         nc.vector.tensor_copy(out=xsg[:], in_=xs[:].indirect(offs_t[:]))
+        for q in range(1, 4):
+            nc.sync.dma_start(out=xsm[32 * q : 32 * q + 4, :].bitcast(I32), in_=xsg[4 * q : 4 * q + 4, :].bitcast(I32))
+        nc.vector.tensor_copy(out=xsm[0:4, :].bitcast(I32), in_=xsg[0:4, :].bitcast(I32))
+        w2w = shared.tile([P, N], I32, name="w2w", align_bytes=64, offset=4 * T)
+        nc.sync.dma_start(out=w2w[:], in_=w2_words[0].rearrange("p c r -> p (c r)").bitcast(I32))
 
-        w1g = sb.tile([P, PACK, P, PACK], BF16, name="w1g", align_bytes=64)
+        w1g = sb.tile([P, 2, 2, P, PACK], BF16, name="w1g", align_bytes=64)
         for h in range(2):
-            dst = w1g[:, :, h * (P // 2) : (h + 1) * (P // 2), :].rearrange("p t m j -> p m j t")
-            src = w1_raw[h][:].rearrange("p j (m t) -> p m j t", t=PACK)
+            ms = slice(0, SPLIT) if h == 0 else slice(SPLIT, P)
+            dst = w1g[:, :, :, ms, :].rearrange("p b a m j -> p m j a b")
+            src = w1_raw[:].rearrange("p j (m a b) -> p m j a b", a=2, b=2)[:, ms]
             if h == 0:
                 nc.scalar.copy(out=dst, in_=src)
             else:
                 nc.vector.tensor_copy(out=dst, in_=src)
-        w1q = {
-            1: sb.tile([P, H // 2], U32, name="w1q1", align_bytes=64),
-            0: shared.tile([P, H // 2], U32, name="w1q0", align_bytes=64, offset=5 * N),
-        }
-        w1s = {
-            1: sb.tile([P, H // 2], U8, name="w1s1", align_bytes=64),
-            0: shared.tile([P, H // 2], U8, name="w1s0", align_bytes=64, offset=7 * N),
-        }
-        w1flat = w1g[:].rearrange("p t m j -> p (t m j)")
-
-        def quantise_w1(h):
+        w1q = [sb.tile([P, H // 2], U32, name="w1q%d" % b, align_bytes=64) for b in range(2)]
+        w1s = [sb.tile([P, H // 2], U8, name="w1s%d" % b, align_bytes=64) for b in range(2)]
+        for b in range(2):
             nc.vector.quantize_mx(
-                out=w1q[h][:].bitcast(FP8X4), scales=w1s[h][:], in_=w1flat[:, h * 2 * H : (h + 1) * 2 * H]
+                out=w1q[b][:].bitcast(FP8X4), scales=w1s[b][:], in_=w1g[:, b].rearrange("p a m j -> p (a m j)")
             )
-
-        quantise_w1(1)
 
         xg = sb.tile([P, S], U32, name="xg", align_bytes=64)
         for h in range(2):
@@ -104,8 +96,6 @@ def tile_picked_carry2_none_po_kernel(
                 out=xg[:, h * HALF : (h + 1) * HALF],
                 in_=xw[:].bitcast(U32).indirect(offs_t[:, h * (HALF // 16) : (h + 1) * (HALF // 16)]),
             )
-
-        quantise_w1(0)
 
         w2d = shared.tile([P, N], I32, name="w2d", align_bytes=64, offset=0)
         w2sd = shared.tile([P, N], U8, name="w2sd", align_bytes=64, offset=4 * N)
@@ -117,21 +107,21 @@ def tile_picked_carry2_none_po_kernel(
         )
 
         state = [sb.tile([P, S], F32, name="state%d" % t, align_bytes=64) for t in range(PACK)]
-        for n, t in enumerate(ORDER):
-            m_cols = slice(t % 2 * P, (t % 2 + 1) * P)
-            pieces = [slice(0, HALF), slice(HALF, S)] if n == 0 else [slice(0, S)]
-            for i, cols in enumerate(pieces):
-                acc = psum.tile([P, cols.stop - cols.start], F32, name="y_acc", tag="bank%d" % (n + i + (n > 0)))
-                nc.tensor.matmul_mx(
-                    out=acc[:],
-                    lhsT=w1q[t // 2][:, m_cols].bitcast(FP8X4),
-                    lhsT_scale=w1s[t // 2][:, m_cols],
-                    rhs=xg[:, cols].bitcast(FP8X4),
-                    rhs_scale=xsg[:, cols],
-                    start=True,
-                    stop=True,
-                )
-                nc.scalar.copy(out=state[t][:, cols], in_=acc[:])
+        halves = [slice(0, HALF), slice(HALF, S)]
+        pieces = [(t, cols) for cols in halves for t in ORDER[:2]] + [(t, slice(0, S)) for t in ORDER[2:]]
+        for bank, (t, cols) in enumerate(pieces):
+            m_cols = slice(t // 2 * P, (t // 2 + 1) * P)
+            acc = psum.tile([P, cols.stop - cols.start], F32, name="y_acc", tag="bank%d" % bank)
+            nc.tensor.matmul_mx(
+                out=acc[:],
+                lhsT=w1q[t % 2][:, m_cols].bitcast(FP8X4),
+                lhsT_scale=w1s[t % 2][:, m_cols],
+                rhs=xg[:, cols].bitcast(FP8X4),
+                rhs_scale=xsm[:, cols],
+                start=True,
+                stop=True,
+            )
+            nc.scalar.copy(out=state[t][:, cols], in_=acc[:])
 
         moved = [sb.tile([P, V], F32, name="moved%d" % t) for t in range(PACK)]
         half_s = {}
@@ -188,7 +178,7 @@ def tile_picked_carry2_none_po_kernel(
             o32 = sb.tile([P, PACK, width], F32, name="o32_%d" % c)
             for i in range(2):
                 pair = slice(2 * i, 2 * i + 2)
-                acc = psum.tile([P, 2, width], F32, name="o_acc", tag="bank%d" % ((5 + 2 * c + i) % 8))
+                acc = psum.tile([P, 2, width], F32, name="o_acc", tag="bank%d" % ((6 + 2 * c + i) % 8))
                 for t in range(pair.start, pair.stop):
                     m_cols = slice(t * P, (t + 1) * P)
                     nc.tensor.matmul_mx(

@@ -44,37 +44,34 @@ def tile_picked_carry2_none_po_kernel(
         s2_t = lists.tile([P, V // 16], U16, name="s2_t")
         d2_t = lists.tile([P, V // 16], U16, name="d2_t")
 
-        xs = shared.tile([P, T], U8, name="xs", align_bytes=64, offset=4 * T)
-        xs_rows = sb.tile([P, T // 4], I32, name="xs_rows", align_bytes=64)
+        xs = sb.tile([P, T], U8, name="xs", align_bytes=64)
         xw = shared.tile([P, T], I32, name="xw", align_bytes=64, offset=0)
         xsm = sb.tile([P, S], U8, name="xsm", align_bytes=64)
         w2s = sb.tile([P, N], U8, name="w2s", align_bytes=64)
-        w1_raw = sb.tile([P, PACK, H], F32, name="w1_raw", align_bytes=64)
+        w1_raw = shared.tile([P, PACK, H], F32, name="w1_raw", align_bytes=64, offset=4 * T)
 
-        nc.vector.memset(xs[:].bitcast(I32), 0)
+        for rows in (slice(0, 16), slice(32, 64), slice(64, P)):
+            nc.vector.memset(xs[rows, :].bitcast(I32), 0)
         nc.gpsimd.memset(xsm[:].bitcast(I32), 0)
         nc.gpsimd.memset(w2s[:].bitcast(I32), 0)
 
-        nc.sync.dma_start(out=xs_rows[0:16, :], in_=x_scales[0].bitcast(I32))
+        nc.scalar.dma_start(out=xs[16:32, :].bitcast(I32), in_=x_scales[0].bitcast(I32))
         nc.sync.dma_start(out=offs_t[:], in_=offs)
         nc.sync.dma_start(out=w1_raw[:], in_=w1.rearrange("(p j) c -> p j c", j=PACK))
         nc.sync.dma_start(out=s1_t[:], in_=s1)
-        nc.sync.dma_start(out=d1_t[:], in_=d1)
         nc.sync.dma_start(out=xw[:], in_=x_words[0].rearrange("p c r -> p (c r)").bitcast(I32))
+        nc.sync.dma_start(out=d1_t[:], in_=d1)
         nc.sync.dma_start(out=s2_t[:], in_=s2)
         nc.sync.dma_start(out=d2_t[:], in_=d2)
         load_scale_rows(nc.gpsimd, w2s[:].bitcast(I32), w2_scales[0])
 
-        nc.vector.tensor_copy(out=xs[0:16, :].bitcast(I32), in_=xs_rows[0:16, :])
         xsg = sb.tile([P, S], U8, name="xsg", align_bytes=64)
         nc.vector.tensor_copy(out=xsg[:], in_=xs[:].indirect(offs_t[:]))
-        for q in range(1, 4):
-            nc.sync.dma_start(out=xsm[32 * q : 32 * q + 4, :].bitcast(I32), in_=xsg[4 * q : 4 * q + 4, :].bitcast(I32))
-        nc.vector.tensor_copy(out=xsm[0:4, :].bitcast(I32), in_=xsg[0:4, :].bitcast(I32))
+        load_scale_rows(nc.sync, xsm[:].bitcast(I32), xsg[16:32, :])
         w2w = shared.tile([P, N], I32, name="w2w", align_bytes=64, offset=4 * T)
         nc.sync.dma_start(out=w2w[:], in_=w2_words[0].rearrange("p c r -> p (c r)").bitcast(I32))
 
-        w1g = sb.tile([P, 2, 2, P, PACK], BF16, name="w1g", align_bytes=64)
+        w1g = shared.tile([P, 2, 2, P, PACK], BF16, name="w1g", align_bytes=64, offset=8 * T)
         for h in range(2):
             ms = slice(0, SPLIT) if h == 0 else slice(SPLIT, P)
             dst = w1g[:, :, :, ms, :].rearrange("p b a m j -> p m j a b")
@@ -90,10 +87,10 @@ def tile_picked_carry2_none_po_kernel(
                 out=w1q[b][:].bitcast(FP8X4), scales=w1s[b][:], in_=w1g[:, b].rearrange("p a m j -> p (a m j)")
             )
 
-        xg = sb.tile([P, S], U32, name="xg", align_bytes=64)
+        xg = [shared.tile([P, HALF], U32, name="xg%d" % h, align_bytes=64, offset=8 * T + 4 * HALF * h) for h in range(2)]
         for h in range(2):
             nc.vector.tensor_copy(
-                out=xg[:, h * HALF : (h + 1) * HALF],
+                out=xg[h][:],
                 in_=xw[:].bitcast(U32).indirect(offs_t[:, h * (HALF // 16) : (h + 1) * (HALF // 16)]),
             )
 
@@ -107,16 +104,16 @@ def tile_picked_carry2_none_po_kernel(
         )
 
         state = [sb.tile([P, S], F32, name="state%d" % t, align_bytes=64) for t in range(PACK)]
-        halves = [slice(0, HALF), slice(HALF, S)]
-        pieces = [(t, cols) for cols in halves for t in ORDER[:2]] + [(t, slice(0, S)) for t in ORDER[2:]]
-        for bank, (t, cols) in enumerate(pieces):
+        pieces = [(t, h) for pair in (ORDER[:2], ORDER[2:]) for h in range(2) for t in pair]
+        for bank, (t, h) in enumerate(pieces):
             m_cols = slice(t // 2 * P, (t // 2 + 1) * P)
-            acc = psum.tile([P, cols.stop - cols.start], F32, name="y_acc", tag="bank%d" % bank)
+            cols = slice(h * HALF, (h + 1) * HALF)
+            acc = psum.tile([P, HALF], F32, name="y_acc", tag="bank%d" % bank)
             nc.tensor.matmul_mx(
                 out=acc[:],
                 lhsT=w1q[t % 2][:, m_cols].bitcast(FP8X4),
                 lhsT_scale=w1s[t % 2][:, m_cols],
-                rhs=xg[:, cols].bitcast(FP8X4),
+                rhs=xg[h][:].bitcast(FP8X4),
                 rhs_scale=xsm[:, cols],
                 start=True,
                 stop=True,
@@ -178,7 +175,7 @@ def tile_picked_carry2_none_po_kernel(
             o32 = sb.tile([P, PACK, width], F32, name="o32_%d" % c)
             for i in range(2):
                 pair = slice(2 * i, 2 * i + 2)
-                acc = psum.tile([P, 2, width], F32, name="o_acc", tag="bank%d" % ((6 + 2 * c + i) % 8))
+                acc = psum.tile([P, 2, width], F32, name="o_acc", tag="bank%d" % (2 * c + i))
                 for t in range(pair.start, pair.stop):
                     m_cols = slice(t * P, (t + 1) * P)
                     nc.tensor.matmul_mx(

@@ -17,10 +17,9 @@ ADD = mybir.AluOpType.add
 
 P = 128
 PACK = 4
-CHUNKS = (slice(0, 128), slice(128, 384), slice(384, 512))
+CHUNKS = tuple(slice(c * P, (c + 1) * P) for c in range(4))
 HALF = S // 2
 ORDER = (0, 2, 3, 1)
-SPLIT = 48
 
 
 def load_scale_rows(queue, tile, rows, quadrants=range(4)):
@@ -67,32 +66,39 @@ def tile_picked_carry2_none_po_kernel(
 
         xsg = sb.tile([P, S], U8, name="xsg", align_bytes=64)
         nc.vector.tensor_copy(out=xsg[:], in_=xs[:].indirect(offs_t[:]))
-        load_scale_rows(nc.sync, xsm[:].bitcast(I32), xsg[16:32, :])
+        load_scale_rows(nc.scalar, xsm[:].bitcast(I32), xsg[16:32, :])
         w2w = shared.tile([P, N], I32, name="w2w", align_bytes=64, offset=4 * T)
         nc.sync.dma_start(out=w2w[:], in_=w2_words[0].rearrange("p c r -> p (c r)").bitcast(I32))
 
-        w1g = shared.tile([P, 2, 2, P, PACK], BF16, name="w1g", align_bytes=64, offset=8 * T)
-        for h in range(2):
-            ms = slice(0, SPLIT) if h == 0 else slice(SPLIT, P)
-            dst = w1g[:, :, :, ms, :].rearrange("p b a m j -> p m j a b")
-            src = w1_raw[:].rearrange("p j (m a b) -> p m j a b", a=2, b=2)[:, ms]
-            if h == 0:
-                nc.scalar.copy(out=dst, in_=src)
-            else:
-                nc.vector.tensor_copy(out=dst, in_=src)
-        w1q = [sb.tile([P, H // 2], U32, name="w1q%d" % b, align_bytes=64) for b in range(2)]
-        w1s = [sb.tile([P, H // 2], U8, name="w1s%d" % b, align_bytes=64) for b in range(2)]
-        for b in range(2):
+        w1g = sb.tile([P, 2, 2, P, PACK], BF16, name="w1g", align_bytes=64)
+        nc.vector.tensor_copy(
+            out=w1g[:].rearrange("p b a m j -> p m j a b"),
+            in_=w1_raw[:].rearrange("p j (m a b) -> p m j a b", a=2, b=2),
+        )
+        w1q = [
+            sb.tile([P, H // 2], U32, name="w1q0", align_bytes=64),
+            shared.tile([P, H // 2], U32, name="w1q1", align_bytes=64, offset=5 * N),
+        ]
+        w1s = [
+            sb.tile([P, H // 2], U8, name="w1s0", align_bytes=64),
+            shared.tile([P, H // 2], U8, name="w1s1", align_bytes=64, offset=7 * N),
+        ]
+
+        def quantise_w1(b):
             nc.vector.quantize_mx(
                 out=w1q[b][:].bitcast(FP8X4), scales=w1s[b][:], in_=w1g[:, b].rearrange("p a m j -> p (a m j)")
             )
 
-        xg = [shared.tile([P, HALF], U32, name="xg%d" % h, align_bytes=64, offset=8 * T + 4 * HALF * h) for h in range(2)]
+        quantise_w1(0)
+
+        xg = [sb.tile([P, HALF], U32, name="xg%d" % h, align_bytes=64) for h in range(2)]
         for h in range(2):
             nc.vector.tensor_copy(
                 out=xg[h][:],
                 in_=xw[:].bitcast(U32).indirect(offs_t[:, h * (HALF // 16) : (h + 1) * (HALF // 16)]),
             )
+
+        quantise_w1(1)
 
         w2d = shared.tile([P, N], I32, name="w2d", align_bytes=64, offset=0)
         w2sd = shared.tile([P, N], U8, name="w2sd", align_bytes=64, offset=4 * N)
@@ -128,6 +134,20 @@ def tile_picked_carry2_none_po_kernel(
             for c, cols in enumerate(CHUNKS)
         ]
 
+        def warm_up(pace):
+            nc.scalar.copy(out=pace, in_=acc[:, 0:1])
+            warm = psum.tile([P, S], F32, name="warm", tag="bank7")
+            for t in range(2):
+                nc.tensor.matmul_mx(
+                    out=warm[:],
+                    lhsT=w2d[:, t * P : (t + 1) * P].bitcast(FP8X4),
+                    lhsT_scale=w2sd[:, t * P : (t + 1) * P],
+                    rhs=w2d[:].bitcast(FP8X4),
+                    rhs_scale=w2sd[:],
+                    start=True,
+                    stop=True,
+                )
+
         def fetch1(t):
             nc.vector.tensor_copy(out=moved[t][:], in_=state[t][:].indirect(s1_t[:]))
 
@@ -145,13 +165,12 @@ def tile_picked_carry2_none_po_kernel(
         def put2(t):
             nc.vector.tensor_tensor(state[t][:].indirect(d2_t[:]), half_s[t][:], half_d[t][:], ADD)
             for c, cols in enumerate(CHUNKS):
-                if t != ORDER[-1]:
+                if t == ORDER[-1] and c < 2:
+                    nc.vector.tensor_copy(out=zb[c][:, :, t], in_=state[t][:, cols])
+                else:
                     nc.scalar.copy(out=zb[c][:, :, t], in_=state[t][:, cols])
-            if t == ORDER[-1]:
-                nc.vector.tensor_copy(out=zb[0][:, :, t], in_=state[t][:, 0:128])
-                nc.vector.tensor_copy(out=zb[1][:, 0:128, t], in_=state[t][:, 128:256])
-                nc.scalar.copy(out=zb[1][:, 128:256, t], in_=state[t][:, 256:384])
-                nc.scalar.copy(out=zb[2][:, :, t], in_=state[t][:, 384:512])
+                if t == ORDER[-2] and c == 0:
+                    warm_up(state[t][:, 0:1])
 
         stages = [fetch1, put1, fetch2, put2]
         for step in range(PACK + len(stages) - 1):
@@ -170,38 +189,58 @@ def tile_picked_carry2_none_po_kernel(
             nc.vector.quantize_mx(
                 out=zq[:, cols].bitcast(FP8X4), scales=zs[:, cols], in_=zb[c][:].rearrange("p n t -> p (n t)")
             )
-        for c, cols in enumerate(CHUNKS):
-            width = cols.stop - cols.start
-            o32 = sb.tile([P, PACK, width], F32, name="o32_%d" % c)
-            for i in range(2):
-                pair = slice(2 * i, 2 * i + 2)
-                acc = psum.tile([P, 2, width], F32, name="o_acc", tag="bank%d" % (2 * c + i))
-                for t in range(pair.start, pair.stop):
-                    m_cols = slice(t * P, (t + 1) * P)
-                    nc.tensor.matmul_mx(
-                        out=acc[:, t - pair.start, :],
-                        lhsT=w2d[:, m_cols].bitcast(FP8X4),
-                        lhsT_scale=w2sd[:, m_cols],
-                        rhs=zq[:, cols].bitcast(FP8X4),
-                        rhs_scale=zs[:, cols],
-                        start=True,
-                        stop=True,
-                    )
-                nc.scalar.copy(out=o32[:, pair, :], in_=acc[:])
-                if c < len(CHUNKS) - 1:
-                    nc.sync.dma_start(out=out_rows[:, pair, cols], in_=o32[:, pair, :])
-            if c == len(CHUNKS) - 1:
-                nc.sync.dma_start(out=out_rows[:, :, cols], in_=o32[:])
-            ob = sb.tile([P, width, PACK], BF16, name="ob%d" % c, align_bytes=64)
+
+        def product(c, planes, bank):
+            cols = CHUNKS[c]
+            o_acc = psum.tile([P, len(planes), P], F32, name="o_acc", tag="bank%d" % bank)
+            for i, t in enumerate(planes):
+                m_cols = slice(t * P, (t + 1) * P)
+                nc.tensor.matmul_mx(
+                    out=o_acc[:, i, :],
+                    lhsT=w2d[:, m_cols].bitcast(FP8X4),
+                    lhsT_scale=w2sd[:, m_cols],
+                    rhs=zq[:, cols].bitcast(FP8X4),
+                    rhs_scale=zs[:, cols],
+                    start=True,
+                    stop=True,
+                )
+            return o_acc
+
+        o32 = sb.tile([P, PACK, S], F32, name="o32", align_bytes=64)
+        ob = [sb.tile([P, HALF, PACK], BF16, name="ob%d" % h, align_bytes=64) for h in range(2)]
+
+        def interleave(c):
             nc.vector.tensor_copy(
-                out=ob[:].rearrange("p (n i) t -> p n t i", i=4), in_=o32[:].rearrange("p t (n i) -> p n t i", i=4)
+                out=ob[c // 2][:, CHUNKS[c % 2], :].rearrange("p (n i) t -> p n t i", i=4),
+                in_=o32[:, :, CHUNKS[c]].rearrange("p t (n i) -> p n t i", i=4),
             )
+
+        def planes_out(h, queue):
+            cols = slice(h * HALF, (h + 1) * HALF)
             nc.vector.quantize_mx(
-                out=oq[:, cols].bitcast(FP8X4), scales=osc[:, cols], in_=ob[:].rearrange("p n t -> p (n t)")
+                out=oq[:, cols].bitcast(FP8X4), scales=osc[:, cols], in_=ob[h][:].rearrange("p n t -> p (n t)")
             )
-            if c > 0:
-                done = slice(0, cols.stop) if c == 1 else cols
-                nc.scalar.dma_start(out=out_words[:, done], in_=oq[:, done].bitcast(I32))
+            queue.dma_start(out=out_words[:, cols], in_=oq[:, cols].bitcast(I32))
+
+        for i in range(2):
+            pair = slice(2 * i, 2 * i + 2)
+            o_acc = product(0, range(pair.start, pair.stop), i)
+            nc.scalar.copy(out=o32[:, pair, CHUNKS[0]], in_=o_acc[:])
+            nc.sync.dma_start(out=out_rows[:, pair, CHUNKS[0]], in_=o32[:, pair, CHUNKS[0]])
+        o_acc = product(1, range(PACK), 2)
+        nc.vector.tensor_copy(out=o32[:, :, CHUNKS[1]], in_=o_acc[:])
+        o_acc = product(2, range(PACK), 3)
+        nc.scalar.copy(out=o32[:, :, CHUNKS[2]], in_=o_acc[:])
+        nc.sync.dma_start(out=out_rows[:, :, P : 3 * P], in_=o32[:, :, P : 3 * P])
+        o_acc = product(3, range(PACK), 4)
+        nc.scalar.copy(out=o32[:, :, CHUNKS[3]], in_=o_acc[:])
+        nc.sync.dma_start(out=out_rows[:, :, CHUNKS[3]], in_=o32[:, :, CHUNKS[3]])
+        nc.scalar.copy(out=ob[1][:, CHUNKS[1], :], in_=o_acc[:].rearrange("p t n -> p n t"))
+        interleave(0)
+        interleave(1)
+        planes_out(0, nc.sync)
+        interleave(2)
+        planes_out(1, nc.scalar)
         for q in range(4):
             queue = nc.scalar if q % 2 == 0 else nc.sync
             queue.dma_start(

@@ -44,37 +44,40 @@ def tile_picked_carry2_none_po_kernel(
         d2_t = lists.tile([P, V // 16], U16, name="d2_t")
 
         xs = sb.tile([P, T], U8, name="xs", align_bytes=64)
+        xs_rows = sb.tile([P, T // 4], I32, name="xs_rows", align_bytes=64)
         xw = shared.tile([P, T], I32, name="xw", align_bytes=64, offset=0)
-        xsm = sb.tile([P, S], U8, name="xsm", align_bytes=64)
         w2s = sb.tile([P, N], U8, name="w2s", align_bytes=64)
-        w1_raw = shared.tile([P, PACK, H], F32, name="w1_raw", align_bytes=64, offset=4 * T)
+        w2w = sb.tile([P, N], I32, name="w2w", align_bytes=64)
+        w1_raw = sb.tile([P, PACK, H], F32, name="w1_raw", align_bytes=64)
 
-        for rows in (slice(0, 16), slice(32, 64), slice(64, P)):
-            nc.vector.memset(xs[rows, :].bitcast(I32), 0)
-        nc.gpsimd.memset(xsm[:].bitcast(I32), 0)
+        nc.vector.memset(xs[:].bitcast(I32), 0)
         nc.gpsimd.memset(w2s[:].bitcast(I32), 0)
 
-        nc.scalar.dma_start(out=xs[16:32, :].bitcast(I32), in_=x_scales[0].bitcast(I32))
+        load_scale_rows(nc.sync, xs_rows, x_scales[0], (0, 1))
+        load_scale_rows(nc.scalar, xs_rows, x_scales[0], (2, 3))
         nc.sync.dma_start(out=offs_t[:], in_=offs)
         nc.sync.dma_start(out=w1_raw[:], in_=w1.rearrange("(p j) c -> p j c", j=PACK))
-        nc.sync.dma_start(out=s1_t[:], in_=s1)
         nc.sync.dma_start(out=xw[:], in_=x_words[0].rearrange("p c r -> p (c r)").bitcast(I32))
+        load_scale_rows(nc.gpsimd, w2s[:].bitcast(I32), w2_scales[0])
+        nc.sync.dma_start(out=s1_t[:], in_=s1)
+        nc.sync.dma_start(out=w2w[:], in_=w2_words[0].rearrange("p c r -> p (c r)").bitcast(I32))
         nc.sync.dma_start(out=d1_t[:], in_=d1)
         nc.sync.dma_start(out=s2_t[:], in_=s2)
         nc.sync.dma_start(out=d2_t[:], in_=d2)
-        load_scale_rows(nc.gpsimd, w2s[:].bitcast(I32), w2_scales[0])
 
+        for q in range(4):
+            rows = slice(32 * q, 32 * q + 4)
+            nc.vector.tensor_copy(out=xs[rows, :].bitcast(I32), in_=xs_rows[rows, :])
         xsg = sb.tile([P, S], U8, name="xsg", align_bytes=64)
         nc.vector.tensor_copy(out=xsg[:], in_=xs[:].indirect(offs_t[:]))
-        load_scale_rows(nc.scalar, xsm[:].bitcast(I32), xsg[16:32, :])
-        w2w = shared.tile([P, N], I32, name="w2w", align_bytes=64, offset=4 * T)
-        nc.sync.dma_start(out=w2w[:], in_=w2_words[0].rearrange("p c r -> p (c r)").bitcast(I32))
 
-        w1g = sb.tile([P, 2, 2, P, PACK], BF16, name="w1g", align_bytes=64)
-        nc.vector.tensor_copy(
-            out=w1g[:].rearrange("p b a m j -> p m j a b"),
-            in_=w1_raw[:].rearrange("p j (m a b) -> p m j a b", a=2, b=2),
-        )
+        w1g = [
+            shared.tile([P, 2, P, PACK], BF16, name="w1g0", align_bytes=64, offset=4 * T),
+            sb.tile([P, 2, P, PACK], BF16, name="w1g1", align_bytes=64),
+        ]
+        raw = w1_raw[:].rearrange("p j (m a b) -> p b m j a", a=2, b=2)
+        nc.vector.tensor_copy(out=w1g[0][:].rearrange("p a m j -> p m j a"), in_=raw[:, 0])
+        nc.scalar.copy(out=w1g[1][:].rearrange("p a m j -> p m j a"), in_=raw[:, 1])
         w1q = [
             sb.tile([P, H // 2], U32, name="w1q0", align_bytes=64),
             shared.tile([P, H // 2], U32, name="w1q1", align_bytes=64, offset=5 * N),
@@ -86,12 +89,12 @@ def tile_picked_carry2_none_po_kernel(
 
         def quantise_w1(b):
             nc.vector.quantize_mx(
-                out=w1q[b][:].bitcast(FP8X4), scales=w1s[b][:], in_=w1g[:, b].rearrange("p a m j -> p (a m j)")
+                out=w1q[b][:].bitcast(FP8X4), scales=w1s[b][:], in_=w1g[b][:].rearrange("p a m j -> p (a m j)")
             )
 
         quantise_w1(0)
 
-        xg = [sb.tile([P, HALF], U32, name="xg%d" % h, align_bytes=64) for h in range(2)]
+        xg = [shared.tile([P, HALF], U32, name="xg%d" % h, align_bytes=64, offset=4 * T + 4 * HALF * h) for h in range(2)]
         for h in range(2):
             nc.vector.tensor_copy(
                 out=xg[h][:],
@@ -120,7 +123,7 @@ def tile_picked_carry2_none_po_kernel(
                 lhsT=w1q[t % 2][:, m_cols].bitcast(FP8X4),
                 lhsT_scale=w1s[t % 2][:, m_cols],
                 rhs=xg[h][:].bitcast(FP8X4),
-                rhs_scale=xsm[:, cols],
+                rhs_scale=xsg[:, cols],
                 start=True,
                 stop=True,
             )

@@ -17,7 +17,7 @@ ADD = mybir.AluOpType.add
 
 P = 128
 PACK = 4
-CHUNKS = tuple(slice(c * P, (c + 1) * P) for c in range(4))
+CHUNKS = (slice(0, 128), slice(128, 384), slice(384, 512))
 HALF = S // 2
 ORDER = (0, 2, 3, 1)
 
@@ -73,18 +73,18 @@ def tile_picked_carry2_none_po_kernel(
 
         w1g = [
             shared.tile([P, 2, P, PACK], BF16, name="w1g0", align_bytes=64, offset=4 * T),
-            sb.tile([P, 2, P, PACK], BF16, name="w1g1", align_bytes=64),
+            shared.tile([P, 2, P, PACK], BF16, name="w1g1", align_bytes=64, offset=5 * T),
         ]
         raw = w1_raw[:].rearrange("p j (m a b) -> p b m j a", a=2, b=2)
-        nc.vector.tensor_copy(out=w1g[0][:].rearrange("p a m j -> p m j a"), in_=raw[:, 0])
-        nc.scalar.copy(out=w1g[1][:].rearrange("p a m j -> p m j a"), in_=raw[:, 1])
+        nc.scalar.copy(out=w1g[0][:].rearrange("p a m j -> p m j a"), in_=raw[:, 0])
+        nc.vector.tensor_copy(out=w1g[1][:].rearrange("p a m j -> p m j a"), in_=raw[:, 1])
         w1q = [
             sb.tile([P, H // 2], U32, name="w1q0", align_bytes=64),
-            shared.tile([P, H // 2], U32, name="w1q1", align_bytes=64, offset=5 * N),
+            sb.tile([P, H // 2], U32, name="w1q1", align_bytes=64),
         ]
         w1s = [
             sb.tile([P, H // 2], U8, name="w1s0", align_bytes=64),
-            shared.tile([P, H // 2], U8, name="w1s1", align_bytes=64, offset=7 * N),
+            sb.tile([P, H // 2], U8, name="w1s1", align_bytes=64),
         ]
 
         def quantise_w1(b):
@@ -93,15 +93,14 @@ def tile_picked_carry2_none_po_kernel(
             )
 
         quantise_w1(0)
+        quantise_w1(1)
 
-        xg = [shared.tile([P, HALF], U32, name="xg%d" % h, align_bytes=64, offset=4 * T + 4 * HALF * h) for h in range(2)]
+        xg = shared.tile([P, S], U32, name="xg", align_bytes=64, offset=4 * T + 2 * S)
         for h in range(2):
             nc.vector.tensor_copy(
-                out=xg[h][:],
+                out=xg[:, h * HALF : (h + 1) * HALF],
                 in_=xw[:].bitcast(U32).indirect(offs_t[:, h * (HALF // 16) : (h + 1) * (HALF // 16)]),
             )
-
-        quantise_w1(1)
 
         w2d = shared.tile([P, N], I32, name="w2d", align_bytes=64, offset=0)
         w2sd = shared.tile([P, N], U8, name="w2sd", align_bytes=64, offset=4 * N)
@@ -113,16 +112,17 @@ def tile_picked_carry2_none_po_kernel(
         )
 
         state = [sb.tile([P, S], F32, name="state%d" % t, align_bytes=64) for t in range(PACK)]
-        pieces = [(t, h) for pair in (ORDER[:2], ORDER[2:]) for h in range(2) for t in pair]
-        for bank, (t, h) in enumerate(pieces):
+        first = ORDER[0]
+        pieces = [(first, slice(0, HALF), 0), (first, slice(HALF, HALF + P), 1), (first, slice(HALF + P, S), 2)]
+        pieces += [(t, slice(0, S), 3 + n) for n, t in enumerate(ORDER[1:])]
+        for t, cols, bank in pieces:
             m_cols = slice(t // 2 * P, (t // 2 + 1) * P)
-            cols = slice(h * HALF, (h + 1) * HALF)
-            acc = psum.tile([P, HALF], F32, name="y_acc", tag="bank%d" % bank)
+            acc = psum.tile([P, cols.stop - cols.start], F32, name="y_acc", tag="bank%d" % bank)
             nc.tensor.matmul_mx(
                 out=acc[:],
                 lhsT=w1q[t % 2][:, m_cols].bitcast(FP8X4),
                 lhsT_scale=w1s[t % 2][:, m_cols],
-                rhs=xg[h][:].bitcast(FP8X4),
+                rhs=xg[:, cols].bitcast(FP8X4),
                 rhs_scale=xsg[:, cols],
                 start=True,
                 stop=True,
@@ -136,20 +136,6 @@ def tile_picked_carry2_none_po_kernel(
             sb.tile([P, cols.stop - cols.start, PACK], BF16, name="zb%d" % c, align_bytes=64)
             for c, cols in enumerate(CHUNKS)
         ]
-
-        def warm_up(pace):
-            nc.scalar.copy(out=pace, in_=acc[:, 0:1])
-            warm = psum.tile([P, S], F32, name="warm", tag="bank7")
-            for t in range(2):
-                nc.tensor.matmul_mx(
-                    out=warm[:],
-                    lhsT=w2d[:, t * P : (t + 1) * P].bitcast(FP8X4),
-                    lhsT_scale=w2sd[:, t * P : (t + 1) * P],
-                    rhs=w2d[:].bitcast(FP8X4),
-                    rhs_scale=w2sd[:],
-                    start=True,
-                    stop=True,
-                )
 
         def fetch1(t):
             nc.vector.tensor_copy(out=moved[t][:], in_=state[t][:].indirect(s1_t[:]))
@@ -168,12 +154,13 @@ def tile_picked_carry2_none_po_kernel(
         def put2(t):
             nc.vector.tensor_tensor(state[t][:].indirect(d2_t[:]), half_s[t][:], half_d[t][:], ADD)
             for c, cols in enumerate(CHUNKS):
-                if t == ORDER[-1] and c < 2:
-                    nc.vector.tensor_copy(out=zb[c][:, :, t], in_=state[t][:, cols])
-                else:
+                if t != ORDER[-1]:
                     nc.scalar.copy(out=zb[c][:, :, t], in_=state[t][:, cols])
-                if t == ORDER[-2] and c == 0:
-                    warm_up(state[t][:, 0:1])
+            if t == ORDER[-1]:
+                nc.vector.tensor_copy(out=zb[0][:, :, t], in_=state[t][:, 0:128])
+                nc.vector.tensor_copy(out=zb[1][:, 0:128, t], in_=state[t][:, 128:256])
+                nc.scalar.copy(out=zb[1][:, 128:256, t], in_=state[t][:, 256:384])
+                nc.scalar.copy(out=zb[2][:, :, t], in_=state[t][:, 384:512])
 
         stages = [fetch1, put1, fetch2, put2]
         for step in range(PACK + len(stages) - 1):
@@ -192,58 +179,38 @@ def tile_picked_carry2_none_po_kernel(
             nc.vector.quantize_mx(
                 out=zq[:, cols].bitcast(FP8X4), scales=zs[:, cols], in_=zb[c][:].rearrange("p n t -> p (n t)")
             )
-
-        def product(c, planes, bank):
-            cols = CHUNKS[c]
-            o_acc = psum.tile([P, len(planes), P], F32, name="o_acc", tag="bank%d" % bank)
-            for i, t in enumerate(planes):
-                m_cols = slice(t * P, (t + 1) * P)
-                nc.tensor.matmul_mx(
-                    out=o_acc[:, i, :],
-                    lhsT=w2d[:, m_cols].bitcast(FP8X4),
-                    lhsT_scale=w2sd[:, m_cols],
-                    rhs=zq[:, cols].bitcast(FP8X4),
-                    rhs_scale=zs[:, cols],
-                    start=True,
-                    stop=True,
-                )
-            return o_acc
-
-        o32 = sb.tile([P, PACK, S], F32, name="o32", align_bytes=64)
-        ob = [sb.tile([P, HALF, PACK], BF16, name="ob%d" % h, align_bytes=64) for h in range(2)]
-
-        def interleave(c):
+        for c, cols in enumerate(CHUNKS):
+            width = cols.stop - cols.start
+            o32 = sb.tile([P, PACK, width], F32, name="o32_%d" % c)
+            for i in range(2):
+                pair = slice(2 * i, 2 * i + 2)
+                acc = psum.tile([P, 2, width], F32, name="o_acc", tag="bank%d" % ((6 + 2 * c + i) % 8))
+                for t in range(pair.start, pair.stop):
+                    m_cols = slice(t * P, (t + 1) * P)
+                    nc.tensor.matmul_mx(
+                        out=acc[:, t - pair.start, :],
+                        lhsT=w2d[:, m_cols].bitcast(FP8X4),
+                        lhsT_scale=w2sd[:, m_cols],
+                        rhs=zq[:, cols].bitcast(FP8X4),
+                        rhs_scale=zs[:, cols],
+                        start=True,
+                        stop=True,
+                    )
+                nc.scalar.copy(out=o32[:, pair, :], in_=acc[:])
+                if c < len(CHUNKS) - 1:
+                    nc.sync.dma_start(out=out_rows[:, pair, cols], in_=o32[:, pair, :])
+            if c == len(CHUNKS) - 1:
+                nc.sync.dma_start(out=out_rows[:, :, cols], in_=o32[:])
+            ob = sb.tile([P, width, PACK], BF16, name="ob%d" % c, align_bytes=64)
             nc.vector.tensor_copy(
-                out=ob[c // 2][:, CHUNKS[c % 2], :].rearrange("p (n i) t -> p n t i", i=4),
-                in_=o32[:, :, CHUNKS[c]].rearrange("p t (n i) -> p n t i", i=4),
+                out=ob[:].rearrange("p (n i) t -> p n t i", i=4), in_=o32[:].rearrange("p t (n i) -> p n t i", i=4)
             )
-
-        def planes_out(h, queue):
-            cols = slice(h * HALF, (h + 1) * HALF)
             nc.vector.quantize_mx(
-                out=oq[:, cols].bitcast(FP8X4), scales=osc[:, cols], in_=ob[h][:].rearrange("p n t -> p (n t)")
+                out=oq[:, cols].bitcast(FP8X4), scales=osc[:, cols], in_=ob[:].rearrange("p n t -> p (n t)")
             )
-            queue.dma_start(out=out_words[:, cols], in_=oq[:, cols].bitcast(I32))
-
-        for i in range(2):
-            pair = slice(2 * i, 2 * i + 2)
-            o_acc = product(0, range(pair.start, pair.stop), i)
-            nc.scalar.copy(out=o32[:, pair, CHUNKS[0]], in_=o_acc[:])
-            nc.sync.dma_start(out=out_rows[:, pair, CHUNKS[0]], in_=o32[:, pair, CHUNKS[0]])
-        o_acc = product(1, range(PACK), 2)
-        nc.vector.tensor_copy(out=o32[:, :, CHUNKS[1]], in_=o_acc[:])
-        o_acc = product(2, range(PACK), 3)
-        nc.scalar.copy(out=o32[:, :, CHUNKS[2]], in_=o_acc[:])
-        nc.sync.dma_start(out=out_rows[:, :, P : 3 * P], in_=o32[:, :, P : 3 * P])
-        o_acc = product(3, range(PACK), 4)
-        nc.scalar.copy(out=o32[:, :, CHUNKS[3]], in_=o_acc[:])
-        nc.sync.dma_start(out=out_rows[:, :, CHUNKS[3]], in_=o32[:, :, CHUNKS[3]])
-        nc.scalar.copy(out=ob[1][:, CHUNKS[1], :], in_=o_acc[:].rearrange("p t n -> p n t"))
-        interleave(0)
-        interleave(1)
-        planes_out(0, nc.sync)
-        interleave(2)
-        planes_out(1, nc.scalar)
+            if c > 0:
+                done = slice(0, cols.stop) if c == 1 else cols
+                nc.scalar.dma_start(out=out_words[:, done], in_=oq[:, done].bitcast(I32))
         for q in range(4):
             queue = nc.scalar if q % 2 == 0 else nc.sync
             queue.dma_start(

@@ -182,9 +182,10 @@ def tile_picked_carry2_none_po_kernel(
         for c, cols in enumerate(CHUNKS):
             width = cols.stop - cols.start
             o32 = sb.tile([P, PACK, width], F32, name="o32_%d" % c)
-            for i in range(2):
-                pair = slice(2 * i, 2 * i + 2)
-                acc = psum.tile([P, 2, width], F32, name="o_acc", tag="bank%d" % ((6 + 2 * c + i) % 8))
+            per_bank = 256 // width
+            for i in range(PACK // per_bank):
+                pair = slice(per_bank * i, per_bank * (i + 1))
+                acc = psum.tile([P, per_bank, width], F32, name="o_acc", tag="bank%d" % ((7 + (0, 2, 6)[c] + i) % 8))
                 for t in range(pair.start, pair.stop):
                     m_cols = slice(t * P, (t + 1) * P)
                     nc.tensor.matmul_mx(
@@ -197,8 +198,9 @@ def tile_picked_carry2_none_po_kernel(
                         stop=True,
                     )
                 nc.scalar.copy(out=o32[:, pair, :], in_=acc[:])
-                if c < len(CHUNKS) - 1:
-                    nc.sync.dma_start(out=out_rows[:, pair, cols], in_=o32[:, pair, :])
+                if c < len(CHUNKS) - 1 and pair.stop % 2 == 0:
+                    rows = slice(pair.stop - 2, pair.stop)
+                    nc.sync.dma_start(out=out_rows[:, rows, cols], in_=o32[:, rows, :])
             if c == len(CHUNKS) - 1:
                 nc.sync.dma_start(out=out_rows[:, :, cols], in_=o32[:])
             ob = sb.tile([P, width, PACK], BF16, name="ob%d" % c, align_bytes=64)

@@ -17,12 +17,21 @@ ADD = mybir.AluOpType.add
 
 P = 128
 PACK = 4
-CHUNKS = (slice(0, 128), slice(128, 384), slice(384, 512))
+QUADRANTS = 4
 HALF = S // 2
+BANKS = 8
+BANK_COLUMNS = 256
+CHUNKS = (slice(0, 128), slice(128, 384), slice(384, 512))
 ORDER = (0, 2, 3, 1)
 
+X_WORDS_AT = 0
+W2_SCALES_AT = 4 * N
+W1_EVEN_AT = 4 * T
+W1_ODD_AT = W1_EVEN_AT + 2 * 2 * P * PACK
+PICKED_AT = W1_ODD_AT - 2 * S
 
-def load_scale_rows(queue, tile, rows, quadrants=range(4)):
+
+def load_scale_rows(queue, tile, rows, quadrants):
     for q in quadrants:
         queue.dma_start(out=tile[32 * q : 32 * q + 4, :], in_=rows[4 * q : 4 * q + 4, :].bitcast(I32))
 
@@ -45,7 +54,7 @@ def tile_picked_carry2_none_po_kernel(
 
         xs = sb.tile([P, T], U8, name="xs", align_bytes=64)
         xs_rows = sb.tile([P, T // 4], I32, name="xs_rows", align_bytes=64)
-        xw = shared.tile([P, T], I32, name="xw", align_bytes=64, offset=0)
+        xw = shared.tile([P, T], I32, name="xw", align_bytes=64, offset=X_WORDS_AT)
         w2s = sb.tile([P, N], U8, name="w2s", align_bytes=64)
         w2w = sb.tile([P, N], I32, name="w2w", align_bytes=64)
         w1_raw = sb.tile([P, PACK, H], F32, name="w1_raw", align_bytes=64)
@@ -58,52 +67,42 @@ def tile_picked_carry2_none_po_kernel(
         nc.sync.dma_start(out=offs_t[:], in_=offs)
         nc.sync.dma_start(out=w1_raw[:], in_=w1.rearrange("(p j) c -> p j c", j=PACK))
         nc.sync.dma_start(out=xw[:], in_=x_words[0].rearrange("p c r -> p (c r)").bitcast(I32))
-        load_scale_rows(nc.gpsimd, w2s[:].bitcast(I32), w2_scales[0])
+        load_scale_rows(nc.gpsimd, w2s[:].bitcast(I32), w2_scales[0], range(QUADRANTS))
         nc.sync.dma_start(out=s1_t[:], in_=s1)
         nc.sync.dma_start(out=w2w[:], in_=w2_words[0].rearrange("p c r -> p (c r)").bitcast(I32))
         nc.sync.dma_start(out=d1_t[:], in_=d1)
         nc.sync.dma_start(out=s2_t[:], in_=s2)
         nc.sync.dma_start(out=d2_t[:], in_=d2)
 
-        for q in range(4):
+        for q in range(QUADRANTS):
             rows = slice(32 * q, 32 * q + 4)
             nc.vector.tensor_copy(out=xs[rows, :].bitcast(I32), in_=xs_rows[rows, :])
         xsg = sb.tile([P, S], U8, name="xsg", align_bytes=64)
         nc.vector.tensor_copy(out=xsg[:], in_=xs[:].indirect(offs_t[:]))
 
         w1g = [
-            shared.tile([P, 2, P, PACK], BF16, name="w1g0", align_bytes=64, offset=4 * T),
-            shared.tile([P, 2, P, PACK], BF16, name="w1g1", align_bytes=64, offset=5 * T),
+            shared.tile([P, 2, P, PACK], BF16, name="w1g0", align_bytes=64, offset=W1_EVEN_AT),
+            shared.tile([P, 2, P, PACK], BF16, name="w1g1", align_bytes=64, offset=W1_ODD_AT),
         ]
         raw = w1_raw[:].rearrange("p j (m a b) -> p b m j a", a=2, b=2)
         nc.scalar.copy(out=w1g[0][:].rearrange("p a m j -> p m j a"), in_=raw[:, 0])
         nc.vector.tensor_copy(out=w1g[1][:].rearrange("p a m j -> p m j a"), in_=raw[:, 1])
-        w1q = [
-            sb.tile([P, H // 2], U32, name="w1q0", align_bytes=64),
-            sb.tile([P, H // 2], U32, name="w1q1", align_bytes=64),
-        ]
-        w1s = [
-            sb.tile([P, H // 2], U8, name="w1s0", align_bytes=64),
-            sb.tile([P, H // 2], U8, name="w1s1", align_bytes=64),
-        ]
-
-        def quantise_w1(b):
+        w1q = [sb.tile([P, H // 2], U32, name="w1q%d" % b, align_bytes=64) for b in range(2)]
+        w1s = [sb.tile([P, H // 2], U8, name="w1s%d" % b, align_bytes=64) for b in range(2)]
+        for b in range(2):
             nc.vector.quantize_mx(
                 out=w1q[b][:].bitcast(FP8X4), scales=w1s[b][:], in_=w1g[b][:].rearrange("p a m j -> p (a m j)")
             )
 
-        quantise_w1(0)
-        quantise_w1(1)
-
-        xg = shared.tile([P, S], U32, name="xg", align_bytes=64, offset=4 * T + 2 * S)
+        xg = shared.tile([P, S], U32, name="xg", align_bytes=64, offset=PICKED_AT)
         for h in range(2):
             nc.vector.tensor_copy(
                 out=xg[:, h * HALF : (h + 1) * HALF],
                 in_=xw[:].bitcast(U32).indirect(offs_t[:, h * (HALF // 16) : (h + 1) * (HALF // 16)]),
             )
 
-        w2d = shared.tile([P, N], I32, name="w2d", align_bytes=64, offset=0)
-        w2sd = shared.tile([P, N], U8, name="w2sd", align_bytes=64, offset=4 * N)
+        w2d = shared.tile([P, N], I32, name="w2d", align_bytes=64, offset=X_WORDS_AT)
+        w2sd = shared.tile([P, N], U8, name="w2sd", align_bytes=64, offset=W2_SCALES_AT)
         nc.vector.tensor_copy(
             out=w2d[:].rearrange("p (t m) -> p m t", t=PACK), in_=w2w[:].rearrange("p (m t) -> p m t", t=PACK)
         )
@@ -112,10 +111,10 @@ def tile_picked_carry2_none_po_kernel(
         )
 
         state = [sb.tile([P, S], F32, name="state%d" % t, align_bytes=64) for t in range(PACK)]
-        first = ORDER[0]
-        pieces = [(first, slice(0, HALF), 0), (first, slice(HALF, HALF + P), 1), (first, slice(HALF + P, S), 2)]
-        pieces += [(t, slice(0, S), 3 + n) for n, t in enumerate(ORDER[1:])]
-        for t, cols, bank in pieces:
+        first, last = ORDER[0], ORDER[-1]
+        pieces = [(first, slice(0, HALF)), (first, slice(HALF, HALF + P)), (first, slice(HALF + P, S))]
+        pieces += [(t, slice(0, S)) for t in ORDER[1:]]
+        for bank, (t, cols) in enumerate(pieces):
             m_cols = slice(t // 2 * P, (t // 2 + 1) * P)
             acc = psum.tile([P, cols.stop - cols.start], F32, name="y_acc", tag="bank%d" % bank)
             nc.tensor.matmul_mx(
@@ -144,8 +143,8 @@ def tile_picked_carry2_none_po_kernel(
             nc.vector.tensor_copy(out=state[t][:].indirect(d1_t[:]), in_=moved[t][:])
 
         def fetch2(t):
-            if t == ORDER[-1]:
-                half_s[t] = sb.tile([P, V], F32, name="half_s_last", tag="state%d" % ORDER[0], align_bytes=64)
+            if t == last:
+                half_s[t] = sb.tile([P, V], F32, name="half_s_last", tag="state%d" % first, align_bytes=64)
             else:
                 half_s[t] = sb.tile([P, V], F32, name="half_s%d" % t)
             nc.vector.tensor_scalar(half_s[t][:], state[t][:].indirect(s2_t[:]), 0.5, 0.0, MULT, ADD)
@@ -153,14 +152,14 @@ def tile_picked_carry2_none_po_kernel(
 
         def put2(t):
             nc.vector.tensor_tensor(state[t][:].indirect(d2_t[:]), half_s[t][:], half_d[t][:], ADD)
-            for c, cols in enumerate(CHUNKS):
-                if t != ORDER[-1]:
+            if t != last:
+                for c, cols in enumerate(CHUNKS):
                     nc.scalar.copy(out=zb[c][:, :, t], in_=state[t][:, cols])
-            if t == ORDER[-1]:
-                nc.vector.tensor_copy(out=zb[0][:, :, t], in_=state[t][:, 0:128])
-                nc.vector.tensor_copy(out=zb[1][:, 0:128, t], in_=state[t][:, 128:256])
-                nc.scalar.copy(out=zb[1][:, 128:256, t], in_=state[t][:, 256:384])
-                nc.scalar.copy(out=zb[2][:, :, t], in_=state[t][:, 384:512])
+            else:
+                nc.vector.tensor_copy(out=zb[0][:, :, t], in_=state[t][:, CHUNKS[0]])
+                nc.vector.tensor_copy(out=zb[1][:, 0:P, t], in_=state[t][:, CHUNKS[1].start : HALF])
+                nc.scalar.copy(out=zb[1][:, P : 2 * P, t], in_=state[t][:, HALF : CHUNKS[1].stop])
+                nc.scalar.copy(out=zb[2][:, :, t], in_=state[t][:, CHUNKS[2]])
 
         stages = [fetch1, put1, fetch2, put2]
         for step in range(PACK + len(stages) - 1):
@@ -179,17 +178,21 @@ def tile_picked_carry2_none_po_kernel(
             nc.vector.quantize_mx(
                 out=zq[:, cols].bitcast(FP8X4), scales=zs[:, cols], in_=zb[c][:].rearrange("p n t -> p (n t)")
             )
+
+        bank = BANKS - 1
         for c, cols in enumerate(CHUNKS):
             width = cols.stop - cols.start
+            is_last_chunk = c == len(CHUNKS) - 1
             o32 = sb.tile([P, PACK, width], F32, name="o32_%d" % c)
-            per_bank = 256 // width
-            for i in range(PACK // per_bank):
-                pair = slice(per_bank * i, per_bank * (i + 1))
-                acc = psum.tile([P, per_bank, width], F32, name="o_acc", tag="bank%d" % ((7 + (0, 2, 6)[c] + i) % 8))
-                for t in range(pair.start, pair.stop):
+            per_bank = BANK_COLUMNS // width
+            for t0 in range(0, PACK, per_bank):
+                planes = slice(t0, t0 + per_bank)
+                acc = psum.tile([P, per_bank, width], F32, name="o_acc", tag="bank%d" % (bank % BANKS))
+                bank = bank + 1
+                for t in range(planes.start, planes.stop):
                     m_cols = slice(t * P, (t + 1) * P)
                     nc.tensor.matmul_mx(
-                        out=acc[:, t - pair.start, :],
+                        out=acc[:, t - t0, :],
                         lhsT=w2d[:, m_cols].bitcast(FP8X4),
                         lhsT_scale=w2sd[:, m_cols],
                         rhs=zq[:, cols].bitcast(FP8X4),
@@ -197,11 +200,11 @@ def tile_picked_carry2_none_po_kernel(
                         start=True,
                         stop=True,
                     )
-                nc.scalar.copy(out=o32[:, pair, :], in_=acc[:])
-                if c < len(CHUNKS) - 1 and pair.stop % 2 == 0:
-                    rows = slice(pair.stop - 2, pair.stop)
-                    nc.sync.dma_start(out=out_rows[:, rows, cols], in_=o32[:, rows, :])
-            if c == len(CHUNKS) - 1:
+                nc.scalar.copy(out=o32[:, planes, :], in_=acc[:])
+                if not is_last_chunk and planes.stop % 2 == 0:
+                    pair = slice(planes.stop - 2, planes.stop)
+                    nc.sync.dma_start(out=out_rows[:, pair, cols], in_=o32[:, pair, :])
+            if is_last_chunk:
                 nc.sync.dma_start(out=out_rows[:, :, cols], in_=o32[:])
             ob = sb.tile([P, width, PACK], BF16, name="ob%d" % c, align_bytes=64)
             nc.vector.tensor_copy(
@@ -211,10 +214,9 @@ def tile_picked_carry2_none_po_kernel(
                 out=oq[:, cols].bitcast(FP8X4), scales=osc[:, cols], in_=ob[:].rearrange("p n t -> p (n t)")
             )
             if c > 0:
-                done = slice(0, cols.stop) if c == 1 else cols
+                done = cols if is_last_chunk else slice(0, cols.stop)
                 nc.scalar.dma_start(out=out_words[:, done], in_=oq[:, done].bitcast(I32))
-        for q in range(4):
-            queue = nc.scalar if q % 2 == 0 else nc.sync
-            queue.dma_start(
+        for q in range(QUADRANTS):
+            nc.sync.dma_start(
                 out=out_2[0, 4 * q : 4 * q + 4, :].bitcast(I32), in_=osc[32 * q : 32 * q + 4, :].bitcast(I32)
             )

@@ -25,7 +25,6 @@ CHUNKS = (slice(0, 128), slice(128, 384), slice(384, 512))
 ORDER = (0, 2, 3, 1)
 
 X_WORDS_AT = 0
-W2_SCALES_AT = 4 * N
 W1_EVEN_AT = 4 * T
 W1_ODD_AT = W1_EVEN_AT + 2 * 2 * P * PACK
 PICKED_AT = W1_ODD_AT - 2 * S
@@ -102,18 +101,16 @@ def tile_picked_carry2_none_po_kernel(
             )
 
         w2d = shared.tile([P, N], I32, name="w2d", align_bytes=64, offset=X_WORDS_AT)
-        w2sd = shared.tile([P, N], U8, name="w2sd", align_bytes=64, offset=W2_SCALES_AT)
         nc.vector.tensor_copy(
             out=w2d[:].rearrange("p (t m) -> p m t", t=PACK), in_=w2w[:].rearrange("p (m t) -> p m t", t=PACK)
-        )
-        nc.vector.tensor_copy(
-            out=w2sd[:].rearrange("p (t m) -> p m t", t=PACK), in_=w2s[:].rearrange("p (m t) -> p m t", t=PACK)
         )
 
         state = [sb.tile([P, S], F32, name="state%d" % t, align_bytes=64) for t in range(PACK)]
         first, last = ORDER[0], ORDER[-1]
-        pieces = [(first, slice(0, HALF)), (first, slice(HALF, HALF + P)), (first, slice(HALF + P, S))]
-        pieces += [(t, slice(0, S)) for t in ORDER[1:]]
+        second = ORDER[1]
+        pieces = [(first, slice(0, HALF)), (second, slice(0, HALF))]
+        pieces += [(first, slice(HALF, HALF + P)), (first, slice(HALF + P, S)), (second, slice(HALF, S))]
+        pieces += [(t, slice(0, S)) for t in ORDER[2:]]
         for bank, (t, cols) in enumerate(pieces):
             m_cols = slice(t // 2 * P, (t // 2 + 1) * P)
             acc = psum.tile([P, cols.stop - cols.start], F32, name="y_acc", tag="bank%d" % bank)
@@ -126,11 +123,15 @@ def tile_picked_carry2_none_po_kernel(
                 start=True,
                 stop=True,
             )
-            nc.scalar.copy(out=state[t][:, cols], in_=acc[:])
+            if t == second and cols.start == 0:
+                nc.vector.tensor_copy(out=state[t][:, cols], in_=acc[:])
+            else:
+                nc.scalar.copy(out=state[t][:, cols], in_=acc[:])
 
         moved = [sb.tile([P, V], F32, name="moved%d" % t) for t in range(PACK)]
         half_s = {}
-        half_d = [sb.tile([P, V], F32, name="half_d%d" % t) for t in range(PACK)]
+        w2sd = []
+        half_d = [sb.tile([P, V], F32, name="half_d%d" % t, tag="half_d%d" % t, align_bytes=64) for t in range(PACK)]
         zb = [
             sb.tile([P, cols.stop - cols.start, PACK], BF16, name="zb%d" % c, align_bytes=64)
             for c, cols in enumerate(CHUNKS)
@@ -156,16 +157,20 @@ def tile_picked_carry2_none_po_kernel(
                 for c, cols in enumerate(CHUNKS):
                     nc.scalar.copy(out=zb[c][:, :, t], in_=state[t][:, cols])
             else:
+                w2sd.append(sb.tile([P, N], U8, name="w2sd", tag="half_d%d" % ORDER[-2], align_bytes=64))
+                nc.vector.tensor_copy(
+                    out=w2sd[0][:].rearrange("p (t m) -> p m t", t=PACK),
+                    in_=w2s[:].rearrange("p (m t) -> p m t", t=PACK),
+                )
                 nc.vector.tensor_copy(out=zb[0][:, :, t], in_=state[t][:, CHUNKS[0]])
                 nc.vector.tensor_copy(out=zb[1][:, 0:P, t], in_=state[t][:, CHUNKS[1].start : HALF])
                 nc.scalar.copy(out=zb[1][:, P : 2 * P, t], in_=state[t][:, HALF : CHUNKS[1].stop])
                 nc.scalar.copy(out=zb[2][:, :, t], in_=state[t][:, CHUNKS[2]])
 
-        stages = [fetch1, put1, fetch2, put2]
-        for step in range(PACK + len(stages) - 1):
-            for n in reversed(range(PACK)):
-                if 0 <= step - n < len(stages):
-                    stages[step - n](ORDER[n])
+        for pair in (ORDER[:2], ORDER[2:]):
+            for stage in (fetch1, put1, fetch2, put2):
+                for t in pair:
+                    stage(t)
 
         zq = sb.tile([P, S], U32, name="zq", align_bytes=64)
         zs = sb.tile([P, S], U8, name="zs", align_bytes=64)
@@ -194,7 +199,7 @@ def tile_picked_carry2_none_po_kernel(
                     nc.tensor.matmul_mx(
                         out=acc[:, t - t0, :],
                         lhsT=w2d[:, m_cols].bitcast(FP8X4),
-                        lhsT_scale=w2sd[:, m_cols],
+                        lhsT_scale=w2sd[0][:, m_cols],
                         rhs=zq[:, cols].bitcast(FP8X4),
                         rhs_scale=zs[:, cols],
                         start=True,

@@ -25,6 +25,7 @@ CHUNKS = (slice(0, 128), slice(128, 384), slice(384, 512))
 ORDER = (0, 2, 3, 1)
 
 X_WORDS_AT = 0
+W2_SCALES_AT = 4 * N
 W1_EVEN_AT = 4 * T
 W1_ODD_AT = W1_EVEN_AT + 2 * 2 * P * PACK
 PICKED_AT = W1_ODD_AT - 2 * S
@@ -102,8 +103,13 @@ def tile_picked_carry2_none_po_kernel(
 
         w2d = shared.tile([P, N], I32, name="w2d", align_bytes=64, offset=X_WORDS_AT)
         nc.vector.tensor_copy(
-            out=w2d[:].rearrange("p (t m) -> p m t", t=PACK), in_=w2w[:].rearrange("p (m t) -> p m t", t=PACK)
+            out=w2d[:].rearrange("p (t n i) -> p n t i", t=PACK, i=4),
+            in_=w2w[:].rearrange("p (n i t) -> p n t i", t=PACK, i=4),
         )
+
+        w2s_planes = w2s[:].rearrange("p (m t) -> p t m", t=PACK)
+        w2sd = [shared.tile([P, 2, P], U8, name="w2sd0", align_bytes=64, offset=W2_SCALES_AT)]
+        nc.vector.tensor_copy(out=w2sd[0][:], in_=w2s_planes[:, 0:2, :])
 
         state = [sb.tile([P, S], F32, name="state%d" % t, align_bytes=64) for t in range(PACK)]
         first, last = ORDER[0], ORDER[-1]
@@ -130,7 +136,6 @@ def tile_picked_carry2_none_po_kernel(
 
         moved = [sb.tile([P, V], F32, name="moved%d" % t) for t in range(PACK)]
         half_s = {}
-        w2sd = []
         half_d = [sb.tile([P, V], F32, name="half_d%d" % t, tag="half_d%d" % t, align_bytes=64) for t in range(PACK)]
         zb = [
             sb.tile([P, cols.stop - cols.start, PACK], BF16, name="zb%d" % c, align_bytes=64)
@@ -157,11 +162,8 @@ def tile_picked_carry2_none_po_kernel(
                 for c, cols in enumerate(CHUNKS):
                     nc.scalar.copy(out=zb[c][:, :, t], in_=state[t][:, cols])
             else:
-                w2sd.append(sb.tile([P, N], U8, name="w2sd", tag="half_d%d" % ORDER[-2], align_bytes=64))
-                nc.vector.tensor_copy(
-                    out=w2sd[0][:].rearrange("p (t m) -> p m t", t=PACK),
-                    in_=w2s[:].rearrange("p (m t) -> p m t", t=PACK),
-                )
+                w2sd.append(sb.tile([P, 2, P], U8, name="w2sd1", tag="half_d%d" % ORDER[-2], align_bytes=64))
+                nc.vector.tensor_copy(out=w2sd[1][:], in_=w2s_planes[:, 2:4, :])
                 nc.vector.tensor_copy(out=zb[0][:, :, t], in_=state[t][:, CHUNKS[0]])
                 nc.vector.tensor_copy(out=zb[1][:, 0:P, t], in_=state[t][:, CHUNKS[1].start : HALF])
                 nc.scalar.copy(out=zb[1][:, P : 2 * P, t], in_=state[t][:, HALF : CHUNKS[1].stop])
@@ -199,7 +201,7 @@ def tile_picked_carry2_none_po_kernel(
                     nc.tensor.matmul_mx(
                         out=acc[:, t - t0, :],
                         lhsT=w2d[:, m_cols].bitcast(FP8X4),
-                        lhsT_scale=w2sd[0][:, m_cols],
+                        lhsT_scale=w2sd[t // 2][:, t % 2, :],
                         rhs=zq[:, cols].bitcast(FP8X4),
                         rhs_scale=zs[:, cols],
                         start=True,

@@ -28,6 +28,9 @@ X_WORDS_AT = 0
 W2_SCALES_AT = 4 * N
 W1_EVEN_AT = 4 * T
 W1_ODD_AT = W1_EVEN_AT + 2 * 2 * P * PACK
+FIRST_STATE_AT = W1_ODD_AT + 2 * 2 * P * PACK
+THIRD_HALF_AT = FIRST_STATE_AT + 4 * S
+LATE_SCALES_AT = THIRD_HALF_AT - P
 PICKED_AT = W1_ODD_AT - 2 * S
 
 
@@ -111,9 +114,9 @@ def tile_picked_carry2_none_po_kernel(
         w2sd = [shared.tile([P, 2, P], U8, name="w2sd0", align_bytes=64, offset=W2_SCALES_AT)]
         nc.vector.tensor_copy(out=w2sd[0][:], in_=w2s_planes[:, 0:2, :])
 
-        state = [sb.tile([P, S], F32, name="state%d" % t, align_bytes=64) for t in range(PACK)]
-        first, last = ORDER[0], ORDER[-1]
-        second = ORDER[1]
+        first, second, third, last = ORDER
+        state = {t: sb.tile([P, S], F32, name="state%d" % t, align_bytes=64) for t in ORDER[1:]}
+        state[first] = shared.tile([P, S], F32, name="state_first", align_bytes=64, offset=FIRST_STATE_AT)
         pieces = [(first, slice(0, HALF)), (second, slice(0, HALF))]
         pieces += [(first, slice(HALF, HALF + P)), (first, slice(HALF + P, S)), (second, slice(HALF, S))]
         pieces += [(t, slice(0, S)) for t in ORDER[2:]]
@@ -134,45 +137,76 @@ def tile_picked_carry2_none_po_kernel(
             else:
                 nc.scalar.copy(out=state[t][:, cols], in_=acc[:])
 
-        moved = [sb.tile([P, V], F32, name="moved%d" % t) for t in range(PACK)]
-        half_s = {}
-        half_d = [sb.tile([P, V], F32, name="half_d%d" % t, tag="half_d%d" % t, align_bytes=64) for t in range(PACK)]
+        moved = {t: sb.tile([P, V], F32, name="moved%d" % t) for t in ORDER}
+        half_s = {t: sb.tile([P, V], F32, name="half_s%d" % t) for t in ORDER}
+        half_d = {t: sb.tile([P, V], F32, name="half_d%d" % t) for t in ORDER if t != third}
+        half_d[third] = shared.tile([P, V], F32, name="half_d_third", align_bytes=64, offset=THIRD_HALF_AT)
         zb = [
             sb.tile([P, cols.stop - cols.start, PACK], BF16, name="zb%d" % c, align_bytes=64)
             for c, cols in enumerate(CHUNKS)
         ]
+        whole, lower, upper = slice(0, V), slice(0, V // 2), slice(V // 2, V)
+        moved_late = shared.tile([P, V // 2], F32, name="moved_late", align_bytes=64, offset=PICKED_AT)
 
-        def fetch1(t):
-            nc.vector.tensor_copy(out=moved[t][:], in_=state[t][:].indirect(s1_t[:]))
+        def entries(list_tile, part):
+            return list_tile[:, part.start // 16 : part.stop // 16]
 
-        def put1(t):
-            nc.vector.tensor_copy(out=state[t][:].indirect(d1_t[:]), in_=moved[t][:])
+        def fetched(t, part):
+            return moved_late[:] if t == second and part == upper else moved[t][:, part]
 
-        def fetch2(t):
-            if t == last:
-                half_s[t] = sb.tile([P, V], F32, name="half_s_last", tag="state%d" % first, align_bytes=64)
-            else:
-                half_s[t] = sb.tile([P, V], F32, name="half_s%d" % t)
-            nc.vector.tensor_scalar(half_s[t][:], state[t][:].indirect(s2_t[:]), 0.5, 0.0, MULT, ADD)
-            nc.vector.tensor_scalar(half_d[t][:], state[t][:].indirect(d2_t[:]), 0.5, 0.0, MULT, ADD)
+        def fetch1(t, part):
+            nc.vector.tensor_copy(out=fetched(t, part), in_=state[t][:].indirect(entries(s1_t, part)))
 
-        def put2(t):
-            nc.vector.tensor_tensor(state[t][:].indirect(d2_t[:]), half_s[t][:], half_d[t][:], ADD)
+        def put1(t, part):
+            nc.vector.tensor_copy(out=state[t][:].indirect(entries(d1_t, part)), in_=fetched(t, part))
+
+        def fetch_s(t, part):
+            nc.vector.tensor_scalar(half_s[t][:, part], state[t][:].indirect(entries(s2_t, part)), 0.5, 0.0, MULT, ADD)
+
+        def fetch_d(t, part):
+            nc.vector.tensor_scalar(half_d[t][:, part], state[t][:].indirect(entries(d2_t, part)), 0.5, 0.0, MULT, ADD)
+
+        def put2(t, part):
+            nc.vector.tensor_tensor(state[t][:].indirect(entries(d2_t, part)), half_s[t][:, part], half_d[t][:, part], ADD)
+            if part == lower:
+                return
             if t != last:
                 for c, cols in enumerate(CHUNKS):
                     nc.scalar.copy(out=zb[c][:, :, t], in_=state[t][:, cols])
             else:
-                w2sd.append(sb.tile([P, 2, P], U8, name="w2sd1", tag="half_d%d" % ORDER[-2], align_bytes=64))
+                w2sd.append(shared.tile([P, 2, P], U8, name="w2sd1", align_bytes=64, offset=LATE_SCALES_AT))
                 nc.vector.tensor_copy(out=w2sd[1][:], in_=w2s_planes[:, 2:4, :])
                 nc.vector.tensor_copy(out=zb[0][:, :, t], in_=state[t][:, CHUNKS[0]])
                 nc.vector.tensor_copy(out=zb[1][:, 0:P, t], in_=state[t][:, CHUNKS[1].start : HALF])
                 nc.scalar.copy(out=zb[1][:, P : 2 * P, t], in_=state[t][:, HALF : CHUNKS[1].stop])
                 nc.scalar.copy(out=zb[2][:, :, t], in_=state[t][:, CHUNKS[2]])
 
-        for pair in (ORDER[:2], ORDER[2:]):
-            for stage in (fetch1, put1, fetch2, put2):
-                for t in pair:
-                    stage(t)
+        fetch1(first, whole)
+        fetch1(second, lower)
+        put1(first, lower)
+        fetch1(second, upper)
+        put1(first, upper)
+        fetch1(third, whole)
+        put1(second, lower)
+        fetch_s(first, whole)
+        put1(third, lower)
+        fetch1(last, whole)
+        put1(second, upper)
+        fetch_d(first, whole)
+        put1(third, upper)
+        fetch_s(second, whole)
+        put1(last, lower)
+        fetch_d(second, whole)
+        put2(first, lower)
+        fetch_s(third, whole)
+        put1(last, upper)
+        fetch_d(third, whole)
+        put2(first, upper)
+        fetch_s(last, whole)
+        put2(second, whole)
+        fetch_d(last, whole)
+        put2(third, whole)
+        put2(last, whole)
 
         zq = sb.tile([P, S], U32, name="zq", align_bytes=64)
         zs = sb.tile([P, S], U8, name="zs", align_bytes=64)

@@ -137,37 +137,42 @@ def tile_picked_carry2_none_po_kernel(
             else:
                 nc.scalar.copy(out=state[t][:, cols], in_=acc[:])
 
-        moved = {t: sb.tile([P, V], F32, name="moved%d" % t) for t in ORDER}
-        half_s = {t: sb.tile([P, V], F32, name="half_s%d" % t) for t in ORDER}
-        half_d = {t: sb.tile([P, V], F32, name="half_d%d" % t) for t in ORDER if t != third}
-        half_d[third] = shared.tile([P, V], F32, name="half_d_third", align_bytes=64, offset=THIRD_HALF_AT)
+        fetched = {}
         zb = [
             sb.tile([P, cols.stop - cols.start, PACK], BF16, name="zb%d" % c, align_bytes=64)
             for c, cols in enumerate(CHUNKS)
         ]
         whole, lower, upper = slice(0, V), slice(0, V // 2), slice(V // 2, V)
-        moved_late = shared.tile([P, V // 2], F32, name="moved_late", align_bytes=64, offset=PICKED_AT)
 
         def entries(list_tile, part):
             return list_tile[:, part.start // 16 : part.stop // 16]
 
-        def fetched(t, part):
-            return moved_late[:] if t == second and part == upper else moved[t][:, part]
+        def buffer(sort, t, part, tag):
+            tile = shared.tile(
+                [P, part.stop - part.start], F32, name="fetched", align_bytes=64, offset=THIRD_HALF_AT + 128 * int(tag)
+            )
+            for piece in (whole, lower, upper):
+                if part.start <= piece.start and piece.stop <= part.stop:
+                    fetched[sort, t, piece.start, piece.stop] = tile[:, piece.start - part.start : piece.stop - part.start]
+            return tile[:]
 
-        def fetch1(t, part):
-            nc.vector.tensor_copy(out=fetched(t, part), in_=state[t][:].indirect(entries(s1_t, part)))
+        def values(sort, t, part):
+            return fetched[sort, t, part.start, part.stop]
+
+        def fetch1(t, part, tag):
+            nc.vector.tensor_copy(out=buffer("m", t, part, tag), in_=state[t][:].indirect(entries(s1_t, part)))
 
         def put1(t, part):
-            nc.vector.tensor_copy(out=state[t][:].indirect(entries(d1_t, part)), in_=fetched(t, part))
+            nc.vector.tensor_copy(out=state[t][:].indirect(entries(d1_t, part)), in_=values("m", t, part))
 
-        def fetch_s(t, part):
-            nc.vector.tensor_scalar(half_s[t][:, part], state[t][:].indirect(entries(s2_t, part)), 0.5, 0.0, MULT, ADD)
+        def fetch_s(t, part, tag):
+            nc.vector.tensor_scalar(buffer("s", t, part, tag), state[t][:].indirect(entries(s2_t, part)), 0.5, 0.0, MULT, ADD)
 
-        def fetch_d(t, part):
-            nc.vector.tensor_scalar(half_d[t][:, part], state[t][:].indirect(entries(d2_t, part)), 0.5, 0.0, MULT, ADD)
+        def fetch_d(t, part, tag):
+            nc.vector.tensor_scalar(buffer("d", t, part, tag), state[t][:].indirect(entries(d2_t, part)), 0.5, 0.0, MULT, ADD)
 
         def put2(t, part):
-            nc.vector.tensor_tensor(state[t][:].indirect(entries(d2_t, part)), half_s[t][:, part], half_d[t][:, part], ADD)
+            nc.vector.tensor_tensor(state[t][:].indirect(entries(d2_t, part)), values("s", t, part), values("d", t, part), ADD)
             if part == lower:
                 return
             if t != last:
@@ -181,31 +186,34 @@ def tile_picked_carry2_none_po_kernel(
                 nc.scalar.copy(out=zb[1][:, P : 2 * P, t], in_=state[t][:, HALF : CHUNKS[1].stop])
                 nc.scalar.copy(out=zb[2][:, :, t], in_=state[t][:, CHUNKS[2]])
 
-        fetch1(first, whole)
-        fetch1(second, lower)
-        put1(first, lower)
-        fetch1(second, upper)
-        put1(first, upper)
-        fetch1(third, whole)
+        fetch1(first, whole, "8")
+        fetch1(second, whole, "16")
+        put1(first, whole)
         put1(second, lower)
-        fetch_s(first, whole)
-        put1(third, lower)
-        fetch1(last, whole)
+        fetch_s(first, lower, "24")
+        fetch_s(first, upper, "32")
+        fetch_d(first, whole, "36")
         put1(second, upper)
-        fetch_d(first, whole)
-        put1(third, upper)
-        fetch_s(second, whole)
-        put1(last, lower)
-        fetch_d(second, whole)
+        fetch1(third, whole, "8")
         put2(first, lower)
-        fetch_s(third, whole)
-        put1(last, upper)
-        fetch_d(third, whole)
+        fetch_s(second, whole, "44")
+        put1(third, lower)
+        fetch1(last, lower, "21")
         put2(first, upper)
-        fetch_s(last, whole)
-        put2(second, whole)
-        fetch_d(last, whole)
-        put2(third, whole)
+        fetch1(last, upper, "27")
+        put1(third, upper)
+        fetch_d(second, whole, "36")
+        put1(last, lower)
+        fetch_s(third, whole, "0")
+        put2(second, lower)
+        fetch_d(third, lower, "18")
+        put1(last, upper)
+        fetch_d(third, upper, "22")
+        put2(second, upper)
+        fetch_s(last, whole, "52")
+        put2(third, lower)
+        fetch_d(last, whole, "36")
+        put2(third, upper)
         put2(last, whole)
 
         zq = sb.tile([P, S], U32, name="zq", align_bytes=64)

@@ -22,16 +22,29 @@ HALF = S // 2
 BANKS = 8
 BANK_COLUMNS = 256
 CHUNKS = (slice(0, 128), slice(128, 384), slice(384, 512))
-ORDER = (0, 2, 3, 1)
+A, B, C, D = 0, 2, 3, 1
+WHOLE, LOWER, UPPER = slice(0, V), slice(0, V // 2), slice(V // 2, V)
 
 X_WORDS_AT = 0
 W2_SCALES_AT = 4 * N
 W1_EVEN_AT = 4 * T
 W1_ODD_AT = W1_EVEN_AT + 2 * 2 * P * PACK
-FIRST_STATE_AT = W1_ODD_AT + 2 * 2 * P * PACK
-THIRD_HALF_AT = FIRST_STATE_AT + 4 * S
-LATE_SCALES_AT = THIRD_HALF_AT - P
 PICKED_AT = W1_ODD_AT - 2 * S
+STATE_A_AT = W1_ODD_AT + 2 * 2 * P * PACK
+Y_B_AT = STATE_A_AT + 4 * S
+LATE_AT = Y_B_AT + 2 * S
+W2_LATE_SCALES_AT = Y_B_AT - P
+
+EARLY_COLUMNS, LATE_COLUMNS = 928, 640
+S1_A_AT, S1_B_AT, S1_C_AT = 0, 256, 640
+S1_D_AT = S1_B_AT
+D2_A_UPPER_AT = S1_C_AT - 96
+S2_B_AT = D2_A_UPPER_AT + V // 2
+S2_D_AT = S1_A_AT
+D2_D_AT = S2_B_AT
+D2_A_LOWER_AT = 256
+D2_B_AT = D2_A_LOWER_AT - 192
+S2_C_AT = D2_A_LOWER_AT + 64
 
 
 def load_scale_rows(queue, tile, rows, quadrants):
@@ -109,18 +122,17 @@ def tile_picked_carry2_none_po_kernel(
             out=w2d[:].rearrange("p (t n i) -> p n t i", t=PACK, i=4),
             in_=w2w[:].rearrange("p (n i t) -> p n t i", t=PACK, i=4),
         )
-
         w2s_planes = w2s[:].rearrange("p (m t) -> p t m", t=PACK)
-        w2sd = [shared.tile([P, 2, P], U8, name="w2sd0", align_bytes=64, offset=W2_SCALES_AT)]
-        nc.vector.tensor_copy(out=w2sd[0][:], in_=w2s_planes[:, 0:2, :])
+        w2sd_low = shared.tile([P, 2, P], U8, name="w2sd_low", align_bytes=64, offset=W2_SCALES_AT)
+        nc.vector.tensor_copy(out=w2sd_low[:], in_=w2s_planes[:, 0:2, :])
 
-        first, second, third, last = ORDER
-        state = {t: sb.tile([P, S], F32, name="state%d" % t, align_bytes=64) for t in ORDER[1:]}
-        state[first] = shared.tile([P, S], F32, name="state_first", align_bytes=64, offset=FIRST_STATE_AT)
-        pieces = [(first, slice(0, HALF)), (second, slice(0, HALF))]
-        pieces += [(first, slice(HALF, HALF + P)), (first, slice(HALF + P, S)), (second, slice(HALF, S))]
-        pieces += [(t, slice(0, S)) for t in ORDER[2:]]
-        for bank, (t, cols) in enumerate(pieces):
+        state = {t: sb.tile([P, S], F32, name="state%d" % t, align_bytes=64) for t in (B, C, D)}
+        state[A] = shared.tile([P, S], F32, name="state_a", align_bytes=64, offset=STATE_A_AT)
+        y = {C: state[C], D: state[D]}
+        y[A] = sb.tile([P, S], F32, name="y_a", align_bytes=64)
+        y[B] = shared.tile([P, S], F32, name="y_b", align_bytes=64, offset=Y_B_AT)
+
+        def project(bank, t, cols):
             m_cols = slice(t // 2 * P, (t // 2 + 1) * P)
             acc = psum.tile([P, cols.stop - cols.start], F32, name="y_acc", tag="bank%d" % bank)
             nc.tensor.matmul_mx(
@@ -132,89 +144,112 @@ def tile_picked_carry2_none_po_kernel(
                 start=True,
                 stop=True,
             )
-            if t == second and cols.start == 0:
-                nc.vector.tensor_copy(out=state[t][:, cols], in_=acc[:])
-            else:
-                nc.scalar.copy(out=state[t][:, cols], in_=acc[:])
+            return acc
 
-        fetched = {}
+        left, right = slice(0, HALF), slice(HALF, S)
+        nc.scalar.copy(out=y[A][:, left], in_=project(0, A, left)[:])
+        nc.vector.tensor_copy(out=y[B][:, left], in_=project(1, B, left)[:])
+        nc.vector.tensor_copy(out=state[A][:, left], in_=y[A][:, left])
+        pieces = (slice(HALF, HALF + P), slice(HALF + P, S))
+        accs = [project(2 + n, A, cols) for n, cols in enumerate(pieces)]
+        for target in (y[A], state[A]):
+            for acc, cols in zip(accs, pieces):
+                nc.scalar.copy(out=target[:, cols], in_=acc[:])
+        nc.scalar.copy(out=y[B][:, right], in_=project(4, B, right)[:])
+        nc.scalar.copy(out=state[B][:, left], in_=y[B][:, left])
+        nc.scalar.copy(out=y[C][:], in_=project(5, C, slice(0, S))[:])
+        nc.scalar.copy(out=state[B][:, right], in_=y[B][:, right])
+        nc.scalar.copy(out=y[D][:], in_=project(6, D, slice(0, S))[:])
+
+        early = sb.tile([P, EARLY_COLUMNS], F32, name="early")
+        late = shared.tile([P, LATE_COLUMNS], F32, name="late", align_bytes=64, offset=LATE_AT)
         zb = [
             sb.tile([P, cols.stop - cols.start, PACK], BF16, name="zb%d" % c, align_bytes=64)
             for c, cols in enumerate(CHUNKS)
         ]
-        whole, lower, upper = slice(0, V), slice(0, V // 2), slice(V // 2, V)
+        fetched = {}
 
         def entries(list_tile, part):
             return list_tile[:, part.start // 16 : part.stop // 16]
 
-        def buffer(sort, t, part, tag):
-            tile = shared.tile(
-                [P, part.stop - part.start], F32, name="fetched", align_bytes=64, offset=THIRD_HALF_AT + 128 * int(tag)
-            )
-            for piece in (whole, lower, upper):
+        def place(name, t, part, tile, at):
+            for piece in (WHOLE, LOWER, UPPER):
                 if part.start <= piece.start and piece.stop <= part.stop:
-                    fetched[sort, t, piece.start, piece.stop] = tile[:, piece.start - part.start : piece.stop - part.start]
-            return tile[:]
+                    shift = at - part.start
+                    fetched[name, t, piece.start, piece.stop] = tile[:, piece.start + shift : piece.stop + shift]
+            return values(name, t, part)
 
-        def values(sort, t, part):
-            return fetched[sort, t, part.start, part.stop]
+        def values(name, t, part):
+            return fetched[name, t, part.start, part.stop]
 
-        def fetch1(t, part, tag):
-            nc.vector.tensor_copy(out=buffer("m", t, part, tag), in_=state[t][:].indirect(entries(s1_t, part)))
+        def on_y_b(part, at):
+            return shared.tile(
+                [P, part.stop - part.start], F32, name="on_y_b", align_bytes=64, offset=Y_B_AT + 4 * at
+            )
+
+        def fetch_s1(t, part, tile, at):
+            nc.vector.tensor_copy(out=place("s1", t, part, tile, at), in_=y[t][:].indirect(entries(s1_t, part)))
 
         def put1(t, part):
-            nc.vector.tensor_copy(out=state[t][:].indirect(entries(d1_t, part)), in_=values("m", t, part))
+            nc.vector.tensor_copy(out=state[t][:].indirect(entries(d1_t, part)), in_=values("s1", t, part))
 
-        def fetch_s(t, part, tag):
-            nc.vector.tensor_scalar(buffer("s", t, part, tag), state[t][:].indirect(entries(s2_t, part)), 0.5, 0.0, MULT, ADD)
+        def fetch_s2(t, part, tile, at):
+            window = state[t][:].indirect(entries(s2_t, part))
+            nc.vector.tensor_scalar(place("s2", t, part, tile, at), window, 0.5, 0.0, MULT, ADD)
 
-        def fetch_d(t, part, tag):
-            nc.vector.tensor_scalar(buffer("d", t, part, tag), state[t][:].indirect(entries(d2_t, part)), 0.5, 0.0, MULT, ADD)
+        def fetch_d2(t, part, tile, at):
+            window = state[t][:].indirect(entries(d2_t, part))
+            nc.vector.tensor_scalar(place("d2", t, part, tile, at), window, 0.5, 0.0, MULT, ADD)
 
         def put2(t, part):
-            nc.vector.tensor_tensor(state[t][:].indirect(entries(d2_t, part)), values("s", t, part), values("d", t, part), ADD)
-            if part == lower:
-                return
-            if t != last:
-                for c, cols in enumerate(CHUNKS):
-                    nc.scalar.copy(out=zb[c][:, :, t], in_=state[t][:, cols])
-            else:
-                w2sd.append(shared.tile([P, 2, P], U8, name="w2sd1", align_bytes=64, offset=LATE_SCALES_AT))
-                nc.vector.tensor_copy(out=w2sd[1][:], in_=w2s_planes[:, 2:4, :])
-                nc.vector.tensor_copy(out=zb[0][:, :, t], in_=state[t][:, CHUNKS[0]])
-                nc.vector.tensor_copy(out=zb[1][:, 0:P, t], in_=state[t][:, CHUNKS[1].start : HALF])
-                nc.scalar.copy(out=zb[1][:, P : 2 * P, t], in_=state[t][:, HALF : CHUNKS[1].stop])
-                nc.scalar.copy(out=zb[2][:, :, t], in_=state[t][:, CHUNKS[2]])
+            window = state[t][:].indirect(entries(d2_t, part))
+            nc.vector.tensor_tensor(window, values("s2", t, part), values("d2", t, part), ADD)
 
-        fetch1(first, whole, "8")
-        fetch1(second, whole, "16")
-        put1(first, whole)
-        put1(second, lower)
-        fetch_s(first, lower, "24")
-        fetch_s(first, upper, "32")
-        fetch_d(first, whole, "36")
-        put1(second, upper)
-        fetch1(third, whole, "8")
-        put2(first, lower)
-        fetch_s(second, whole, "44")
-        put1(third, lower)
-        fetch1(last, lower, "21")
-        put2(first, upper)
-        fetch1(last, upper, "27")
-        put1(third, upper)
-        fetch_d(second, whole, "36")
-        put1(last, lower)
-        fetch_s(third, whole, "0")
-        put2(second, lower)
-        fetch_d(third, lower, "18")
-        put1(last, upper)
-        fetch_d(third, upper, "22")
-        put2(second, upper)
-        fetch_s(last, whole, "52")
-        put2(third, lower)
-        fetch_d(last, whole, "36")
-        put2(third, upper)
-        put2(last, whole)
+        def round_plane(t):
+            for c, cols in enumerate(CHUNKS):
+                nc.scalar.copy(out=zb[c][:, :, t], in_=state[t][:, cols])
+
+        fetch_s1(A, LOWER, early, S1_A_AT)
+        fetch_s1(A, UPPER, early, S1_A_AT + V // 2)
+        put1(A, LOWER)
+        fetch_s1(B, WHOLE, early, S1_B_AT)
+        put1(A, UPPER)
+        fetch_s1(C, WHOLE, early, S1_C_AT)
+        put1(B, LOWER)
+        fetch_s2(A, WHOLE, on_y_b(WHOLE, 0), 0)
+        put1(C, LOWER)
+        fetch_d2(A, LOWER, late, D2_A_LOWER_AT)
+        put1(B, UPPER)
+        fetch_d2(A, UPPER, early, D2_A_UPPER_AT)
+        put1(C, UPPER)
+        fetch_s1(D, WHOLE, early, S1_D_AT)
+        put2(A, LOWER)
+        fetch_s2(B, WHOLE, early, S2_B_AT)
+        put1(D, LOWER)
+        fetch_d2(B, WHOLE, late, D2_B_AT)
+        put2(A, UPPER)
+        round_plane(A)
+        fetch_s2(C, WHOLE, late, S2_C_AT)
+        put2(B, LOWER)
+        fetch_d2(C, LOWER, on_y_b(LOWER, V // 2), 0)
+        put1(D, UPPER)
+        fetch_d2(C, UPPER, on_y_b(UPPER, 0), 0)
+        put2(B, UPPER)
+        round_plane(B)
+        fetch_s2(D, WHOLE, early, S2_D_AT)
+        put2(C, LOWER)
+        fetch_d2(D, WHOLE, early, D2_D_AT)
+        put2(C, UPPER)
+        round_plane(C)
+        put2(D, WHOLE)
+
+        w2sd_high = shared.tile([P, 2, P], U8, name="w2sd_high", align_bytes=64, offset=W2_LATE_SCALES_AT)
+        nc.vector.tensor_copy(out=w2sd_high[:], in_=w2s_planes[:, 2:4, :])
+        w2sd = (w2sd_low, w2sd_high)
+        nc.vector.tensor_copy(out=zb[0][:, :, D], in_=state[D][:, CHUNKS[0]])
+        nc.vector.tensor_copy(out=zb[1][:, 0:P, D], in_=state[D][:, CHUNKS[1].start : HALF])
+        nc.scalar.copy(out=zb[1][:, P : 2 * P, D], in_=state[D][:, HALF : CHUNKS[1].stop])
+        nc.scalar.copy(out=zb[2][:, :, D], in_=state[D][:, CHUNKS[2]])
 
         zq = sb.tile([P, S], U32, name="zq", align_bytes=64)
         zs = sb.tile([P, S], U8, name="zs", align_bytes=64)

@@ -12,15 +12,15 @@ U32 = mybir.dt.uint32
 U16 = mybir.dt.uint16
 U8 = mybir.dt.uint8
 FP8X4 = mybir.dt.float8_e4m3fn_x4
-MULT = mybir.AluOpType.mult
 ADD = mybir.AluOpType.add
+COPY = mybir.ActivationFunctionType.Copy
 
 P = 128
 PACK = 4
 QUADRANTS = 4
-HALF = S // 2
 BANKS = 8
 BANK_COLUMNS = 256
+PIECES = (slice(0, 256), slice(256, 384), slice(384, 512))
 CHUNKS = (slice(0, 128), slice(128, 384), slice(384, 512))
 A, B, C, D = 0, 2, 3, 1
 WHOLE, LOWER, UPPER = slice(0, V), slice(0, V // 2), slice(V // 2, V)
@@ -30,21 +30,6 @@ W2_SCALES_AT = 4 * N
 W1_EVEN_AT = 4 * T
 W1_ODD_AT = W1_EVEN_AT + 2 * 2 * P * PACK
 PICKED_AT = W1_ODD_AT - 2 * S
-STATE_A_AT = W1_ODD_AT + 2 * 2 * P * PACK
-Y_B_AT = STATE_A_AT + 4 * S
-LATE_AT = Y_B_AT + 2 * S
-W2_LATE_SCALES_AT = Y_B_AT - P
-
-EARLY_COLUMNS, LATE_COLUMNS = 928, 640
-S1_A_AT, S1_B_AT, S1_C_AT = 0, 256, 640
-S1_D_AT = S1_B_AT
-D2_A_UPPER_AT = S1_C_AT - 96
-S2_B_AT = D2_A_UPPER_AT + V // 2
-S2_D_AT = S1_A_AT
-D2_D_AT = S2_B_AT
-D2_A_LOWER_AT = 256
-D2_B_AT = D2_A_LOWER_AT - 192
-S2_C_AT = D2_A_LOWER_AT + 64
 
 
 def load_scale_rows(queue, tile, rows, quadrants):
@@ -90,6 +75,9 @@ def tile_picked_carry2_none_po_kernel(
         nc.sync.dma_start(out=s2_t[:], in_=s2)
         nc.sync.dma_start(out=d2_t[:], in_=d2)
 
+        def entries(list_tile, part):
+            return list_tile[:, part.start // 16 : part.stop // 16]
+
         for q in range(QUADRANTS):
             rows = slice(32 * q, 32 * q + 4)
             nc.vector.tensor_copy(out=xs[rows, :].bitcast(I32), in_=xs_rows[rows, :])
@@ -111,26 +99,18 @@ def tile_picked_carry2_none_po_kernel(
             )
 
         xg = shared.tile([P, S], U32, name="xg", align_bytes=64, offset=PICKED_AT)
-        for h in range(2):
-            nc.vector.tensor_copy(
-                out=xg[:, h * HALF : (h + 1) * HALF],
-                in_=xw[:].bitcast(U32).indirect(offs_t[:, h * (HALF // 16) : (h + 1) * (HALF // 16)]),
-            )
+        for cols in PIECES:
+            nc.vector.tensor_copy(out=xg[:, cols], in_=xw[:].bitcast(U32).indirect(entries(offs_t, cols)))
 
         w2d = shared.tile([P, N], I32, name="w2d", align_bytes=64, offset=X_WORDS_AT)
         nc.vector.tensor_copy(
             out=w2d[:].rearrange("p (t n i) -> p n t i", t=PACK, i=4),
             in_=w2w[:].rearrange("p (n i t) -> p n t i", t=PACK, i=4),
         )
-        w2s_planes = w2s[:].rearrange("p (m t) -> p t m", t=PACK)
-        w2sd_low = shared.tile([P, 2, P], U8, name="w2sd_low", align_bytes=64, offset=W2_SCALES_AT)
-        nc.vector.tensor_copy(out=w2sd_low[:], in_=w2s_planes[:, 0:2, :])
+        w2sd = shared.tile([P, PACK, P], U8, name="w2sd", align_bytes=64, offset=W2_SCALES_AT)
+        nc.vector.tensor_copy(out=w2sd[:], in_=w2s[:].rearrange("p (m t) -> p t m", t=PACK))
 
-        state = {t: sb.tile([P, S], F32, name="state%d" % t, align_bytes=64) for t in (B, C, D)}
-        state[A] = shared.tile([P, S], F32, name="state_a", align_bytes=64, offset=STATE_A_AT)
-        y = {C: state[C], D: state[D]}
-        y[A] = sb.tile([P, S], F32, name="y_a", align_bytes=64)
-        y[B] = shared.tile([P, S], F32, name="y_b", align_bytes=64, offset=Y_B_AT)
+        state = [sb.tile([P, S], F32, name="state%d" % t, align_bytes=64) for t in range(PACK)]
 
         def project(bank, t, cols):
             m_cols = slice(t // 2 * P, (t // 2 + 1) * P)
@@ -146,109 +126,72 @@ def tile_picked_carry2_none_po_kernel(
             )
             return acc
 
-        left, right = slice(0, HALF), slice(HALF, S)
-        nc.scalar.copy(out=y[A][:, left], in_=project(0, A, left)[:])
-        nc.vector.tensor_copy(out=y[B][:, left], in_=project(1, B, left)[:])
-        nc.vector.tensor_copy(out=state[A][:, left], in_=y[A][:, left])
-        pieces = (slice(HALF, HALF + P), slice(HALF + P, S))
-        accs = [project(2 + n, A, cols) for n, cols in enumerate(pieces)]
-        for target in (y[A], state[A]):
-            for acc, cols in zip(accs, pieces):
-                nc.scalar.copy(out=target[:, cols], in_=acc[:])
-        nc.scalar.copy(out=y[B][:, right], in_=project(4, B, right)[:])
-        nc.scalar.copy(out=state[B][:, left], in_=y[B][:, left])
-        nc.scalar.copy(out=y[C][:], in_=project(5, C, slice(0, S))[:])
-        nc.scalar.copy(out=state[B][:, right], in_=y[B][:, right])
-        nc.scalar.copy(out=y[D][:], in_=project(6, D, slice(0, S))[:])
+        for bank, cols in enumerate(PIECES):
+            nc.scalar.copy(out=state[A][:, cols], in_=project(bank, A, cols)[:])
+        left, right = slice(0, S // 2), slice(S // 2, S)
 
-        early = sb.tile([P, EARLY_COLUMNS], F32, name="early")
-        late = shared.tile([P, LATE_COLUMNS], F32, name="late", align_bytes=64, offset=LATE_AT)
+        by_s1 = [sb.tile([P, V], F32, name="by_s1_%d" % t) for t in range(PACK)]
+        by_s2 = [sb.tile([P, V], F32, name="by_s2_%d" % t) for t in range(PACK)]
+        by_d2 = [sb.tile([P, V], F32, name="by_d2_%d" % t) for t in range(PACK)]
         zb = [
             sb.tile([P, cols.stop - cols.start, PACK], BF16, name="zb%d" % c, align_bytes=64)
             for c, cols in enumerate(CHUNKS)
         ]
-        fetched = {}
 
-        def entries(list_tile, part):
-            return list_tile[:, part.start // 16 : part.stop // 16]
+        y_acc = {}
 
-        def place(name, t, part, tile, at):
-            for piece in (WHOLE, LOWER, UPPER):
-                if part.start <= piece.start and piece.stop <= part.stop:
-                    shift = at - part.start
-                    fetched[name, t, piece.start, piece.stop] = tile[:, piece.start + shift : piece.stop + shift]
-            return values(name, t, part)
+        def empty(t, cols):
+            nc.scalar.copy(out=state[t][:, cols], in_=y_acc[t][:, cols])
 
-        def values(name, t, part):
-            return fetched[name, t, part.start, part.stop]
+        def fetch1(t, part):
+            nc.scalar.activation(by_s1[t][:, part], state[t][:].indirect(entries(s1_t, part)), COPY)
 
-        def on_y_b(part, at):
-            return shared.tile(
-                [P, part.stop - part.start], F32, name="on_y_b", align_bytes=64, offset=Y_B_AT + 4 * at
-            )
+        def put1(t):
+            nc.vector.tensor_copy(out=state[t][:].indirect(d1_t[:]), in_=by_s1[t][:])
 
-        def fetch_s1(t, part, tile, at):
-            nc.vector.tensor_copy(out=place("s1", t, part, tile, at), in_=y[t][:].indirect(entries(s1_t, part)))
+        def fetch2(t):
+            nc.scalar.activation(by_s2[t][:], state[t][:].indirect(s2_t[:]), COPY, scale=0.5)
+            nc.scalar.activation(by_d2[t][:], state[t][:].indirect(d2_t[:]), COPY, scale=0.5)
 
-        def put1(t, part):
-            nc.vector.tensor_copy(out=state[t][:].indirect(entries(d1_t, part)), in_=values("s1", t, part))
-
-        def fetch_s2(t, part, tile, at):
-            window = state[t][:].indirect(entries(s2_t, part))
-            nc.vector.tensor_scalar(place("s2", t, part, tile, at), window, 0.5, 0.0, MULT, ADD)
-
-        def fetch_d2(t, part, tile, at):
-            window = state[t][:].indirect(entries(d2_t, part))
-            nc.vector.tensor_scalar(place("d2", t, part, tile, at), window, 0.5, 0.0, MULT, ADD)
-
-        def put2(t, part):
-            window = state[t][:].indirect(entries(d2_t, part))
-            nc.vector.tensor_tensor(window, values("s2", t, part), values("d2", t, part), ADD)
+        def put2(t):
+            nc.vector.tensor_tensor(state[t][:].indirect(d2_t[:]), by_s2[t][:], by_d2[t][:], ADD)
 
         def round_plane(t):
             for c, cols in enumerate(CHUNKS):
                 nc.scalar.copy(out=zb[c][:, :, t], in_=state[t][:, cols])
 
-        fetch_s1(A, LOWER, early, S1_A_AT)
-        fetch_s1(A, UPPER, early, S1_A_AT + V // 2)
-        put1(A, LOWER)
-        fetch_s1(B, WHOLE, early, S1_B_AT)
-        put1(A, UPPER)
-        fetch_s1(C, WHOLE, early, S1_C_AT)
-        put1(B, LOWER)
-        fetch_s2(A, WHOLE, on_y_b(WHOLE, 0), 0)
-        put1(C, LOWER)
-        fetch_d2(A, LOWER, late, D2_A_LOWER_AT)
-        put1(B, UPPER)
-        fetch_d2(A, UPPER, early, D2_A_UPPER_AT)
-        put1(C, UPPER)
-        fetch_s1(D, WHOLE, early, S1_D_AT)
-        put2(A, LOWER)
-        fetch_s2(B, WHOLE, early, S2_B_AT)
-        put1(D, LOWER)
-        fetch_d2(B, WHOLE, late, D2_B_AT)
-        put2(A, UPPER)
+        nc.vector.tensor_copy(out=by_s1[A][:, LOWER], in_=state[A][:].indirect(entries(s1_t, LOWER)))
+        fetch1(A, UPPER)
+        put1(A)
+        y_acc[B] = project(1, B, slice(0, S))
+        y_acc[C] = project(2, C, slice(0, S))
+        empty(B, slice(0, S))
+        y_acc[D] = project(1, D, slice(0, S))
+        empty(C, left)
+        fetch1(B, WHOLE)
+        put1(B)
+        empty(C, right)
+        empty(D, left)
+        fetch1(C, WHOLE)
+        put1(C)
+        empty(D, right)
+        fetch2(A)
+        put2(A)
+        fetch1(D, WHOLE)
+        put1(D)
+        fetch2(B)
+        put2(B)
+        fetch2(C)
         round_plane(A)
-        fetch_s2(C, WHOLE, late, S2_C_AT)
-        put2(B, LOWER)
-        fetch_d2(C, LOWER, on_y_b(LOWER, V // 2), 0)
-        put1(D, UPPER)
-        fetch_d2(C, UPPER, on_y_b(UPPER, 0), 0)
-        put2(B, UPPER)
+        put2(C)
+        fetch2(D)
         round_plane(B)
-        fetch_s2(D, WHOLE, early, S2_D_AT)
-        put2(C, LOWER)
-        fetch_d2(D, WHOLE, early, D2_D_AT)
-        put2(C, UPPER)
+        put2(D)
         round_plane(C)
-        put2(D, WHOLE)
 
-        w2sd_high = shared.tile([P, 2, P], U8, name="w2sd_high", align_bytes=64, offset=W2_LATE_SCALES_AT)
-        nc.vector.tensor_copy(out=w2sd_high[:], in_=w2s_planes[:, 2:4, :])
-        w2sd = (w2sd_low, w2sd_high)
         nc.vector.tensor_copy(out=zb[0][:, :, D], in_=state[D][:, CHUNKS[0]])
-        nc.vector.tensor_copy(out=zb[1][:, 0:P, D], in_=state[D][:, CHUNKS[1].start : HALF])
-        nc.scalar.copy(out=zb[1][:, P : 2 * P, D], in_=state[D][:, HALF : CHUNKS[1].stop])
+        nc.vector.tensor_copy(out=zb[1][:, 0:P, D], in_=state[D][:, CHUNKS[1].start : S // 2])
+        nc.scalar.copy(out=zb[1][:, P : 2 * P, D], in_=state[D][:, S // 2 : CHUNKS[1].stop])
         nc.scalar.copy(out=zb[2][:, :, D], in_=state[D][:, CHUNKS[2]])
 
         zq = sb.tile([P, S], U32, name="zq", align_bytes=64)
@@ -278,7 +221,7 @@ def tile_picked_carry2_none_po_kernel(
                     nc.tensor.matmul_mx(
                         out=acc[:, t - t0, :],
                         lhsT=w2d[:, m_cols].bitcast(FP8X4),
-                        lhsT_scale=w2sd[t // 2][:, t % 2, :],
+                        lhsT_scale=w2sd[:, t, :],
                         rhs=zq[:, cols].bitcast(FP8X4),
                         rhs_scale=zs[:, cols],
                         start=True,

@@ -30,6 +30,7 @@ W2_SCALES_AT = 4 * N
 W1_EVEN_AT = 4 * T
 W1_ODD_AT = W1_EVEN_AT + 2 * 2 * P * PACK
 PICKED_AT = W1_ODD_AT - 2 * S
+STATES_AT, STATE_PITCH = 32 * 1024, 48 * 1024
 
 
 def load_scale_rows(queue, tile, rows, quadrants):
@@ -110,7 +111,10 @@ def tile_picked_carry2_none_po_kernel(
         w2sd = shared.tile([P, PACK, P], U8, name="w2sd", align_bytes=64, offset=W2_SCALES_AT)
         nc.vector.tensor_copy(out=w2sd[:], in_=w2s[:].rearrange("p (m t) -> p t m", t=PACK))
 
-        state = [sb.tile([P, S], F32, name="state%d" % t, align_bytes=64) for t in range(PACK)]
+        state = [
+            shared.tile([P, S], F32, name="state%d" % t, align_bytes=64, offset=STATES_AT + t * STATE_PITCH)
+            for t in range(PACK)
+        ]
 
         def project(bank, t, cols):
             m_cols = slice(t // 2 * P, (t // 2 + 1) * P)
@@ -129,6 +133,7 @@ def tile_picked_carry2_none_po_kernel(
         for bank, cols in enumerate(PIECES):
             nc.scalar.copy(out=state[A][:, cols], in_=project(bank, A, cols)[:])
         left, right = slice(0, S // 2), slice(S // 2, S)
+        nc.vector.tensor_copy(out=state[B][:, left], in_=project(len(PIECES), B, left)[:])
 
         by_s1 = [sb.tile([P, V], F32, name="by_s1_%d" % t) for t in range(PACK)]
         by_s2 = [sb.tile([P, V], F32, name="by_s2_%d" % t) for t in range(PACK)]
@@ -163,10 +168,10 @@ def tile_picked_carry2_none_po_kernel(
         nc.vector.tensor_copy(out=by_s1[A][:, LOWER], in_=state[A][:].indirect(entries(s1_t, LOWER)))
         fetch1(A, UPPER)
         put1(A)
-        y_acc[B] = project(1, B, slice(0, S))
-        y_acc[C] = project(2, C, slice(0, S))
-        empty(B, slice(0, S))
-        y_acc[D] = project(1, D, slice(0, S))
+        b_right = project(0, B, right)
+        y_acc[C] = project(1, C, slice(0, S))
+        nc.scalar.copy(out=state[B][:, right], in_=b_right[:])
+        y_acc[D] = project(0, D, slice(0, S))
         empty(C, left)
         fetch1(B, WHOLE)
         put1(B)
@@ -207,10 +212,12 @@ def tile_picked_carry2_none_po_kernel(
             )
 
         bank = BANKS - 1
+        results = []
         for c, cols in enumerate(CHUNKS):
             width = cols.stop - cols.start
             is_last_chunk = c == len(CHUNKS) - 1
             o32 = sb.tile([P, PACK, width], F32, name="o32_%d" % c)
+            results.append(o32)
             per_bank = BANK_COLUMNS // width
             for t0 in range(0, PACK, per_bank):
                 planes = slice(t0, t0 + per_bank)
@@ -233,6 +240,10 @@ def tile_picked_carry2_none_po_kernel(
                     nc.sync.dma_start(out=out_rows[:, pair, cols], in_=o32[:, pair, :])
             if is_last_chunk:
                 nc.sync.dma_start(out=out_rows[:, :, cols], in_=o32[:])
+
+        for c, (cols, o32) in enumerate(zip(CHUNKS, results)):
+            width = cols.stop - cols.start
+            is_last_chunk = c == len(CHUNKS) - 1
             ob = sb.tile([P, width, PACK], BF16, name="ob%d" % c, align_bytes=64)
             nc.vector.tensor_copy(
                 out=ob[:].rearrange("p (n i) t -> p n t i", i=4), in_=o32[:].rearrange("p t (n i) -> p n t i", i=4)

@@ -29,7 +29,9 @@ X_WORDS_AT = 0
 W2_SCALES_AT = 4 * N
 W1_EVEN_AT = 4 * T
 W1_ODD_AT = W1_EVEN_AT + 2 * 2 * P * PACK
-PICKED_AT = W1_ODD_AT - 2 * S
+PICKED_AT = W1_EVEN_AT
+W1_ODD_CODES_AT = 4 * N + N
+BY_S1_B_AT = W1_ODD_AT + 2 * 2 * P * PACK
 STATES_AT, STATE_PITCH = 32 * 1024, 48 * 1024
 
 
@@ -90,24 +92,26 @@ def tile_picked_carry2_none_po_kernel(
             shared.tile([P, 2, P, PACK], BF16, name="w1g1", align_bytes=64, offset=W1_ODD_AT),
         ]
         raw = w1_raw[:].rearrange("p j (m a b) -> p b m j a", a=2, b=2)
-        nc.scalar.copy(out=w1g[0][:].rearrange("p a m j -> p m j a"), in_=raw[:, 0])
-        nc.vector.tensor_copy(out=w1g[1][:].rearrange("p a m j -> p m j a"), in_=raw[:, 1])
-        w1q = [sb.tile([P, H // 2], U32, name="w1q%d" % b, align_bytes=64) for b in range(2)]
+        nc.vector.tensor_copy(out=w1g[0][:].rearrange("p a m j -> p m j a"), in_=raw[:, 0])
+        nc.scalar.copy(out=w1g[1][:].rearrange("p a m j -> p m j a"), in_=raw[:, 1])
+        w1q = [
+            sb.tile([P, H // 2], U32, name="w1q0", align_bytes=64),
+            shared.tile([P, H // 2], U32, name="w1q1", align_bytes=64, offset=W1_ODD_CODES_AT),
+        ]
         w1s = [sb.tile([P, H // 2], U8, name="w1s%d" % b, align_bytes=64) for b in range(2)]
-        for b in range(2):
+
+        def quantise_w1(b):
             nc.vector.quantize_mx(
                 out=w1q[b][:].bitcast(FP8X4), scales=w1s[b][:], in_=w1g[b][:].rearrange("p a m j -> p (a m j)")
             )
+
+        quantise_w1(0)
 
         xg = shared.tile([P, S], U32, name="xg", align_bytes=64, offset=PICKED_AT)
         for cols in PIECES:
             nc.vector.tensor_copy(out=xg[:, cols], in_=xw[:].bitcast(U32).indirect(entries(offs_t, cols)))
 
-        w2d = shared.tile([P, N], I32, name="w2d", align_bytes=64, offset=X_WORDS_AT)
-        nc.vector.tensor_copy(
-            out=w2d[:].rearrange("p (t n i) -> p n t i", t=PACK, i=4),
-            in_=w2w[:].rearrange("p (n i t) -> p n t i", t=PACK, i=4),
-        )
+        quantise_w1(1)
         w2sd = shared.tile([P, PACK, P], U8, name="w2sd", align_bytes=64, offset=W2_SCALES_AT)
         nc.vector.tensor_copy(out=w2sd[:], in_=w2s[:].rearrange("p (m t) -> p t m", t=PACK))
 
@@ -135,7 +139,8 @@ def tile_picked_carry2_none_po_kernel(
         left, right = slice(0, S // 2), slice(S // 2, S)
         nc.vector.tensor_copy(out=state[B][:, left], in_=project(len(PIECES), B, left)[:])
 
-        by_s1 = [sb.tile([P, V], F32, name="by_s1_%d" % t) for t in range(PACK)]
+        by_s1 = {t: sb.tile([P, V], F32, name="by_s1_%d" % t) for t in (A, C, D)}
+        by_s1[B] = shared.tile([P, V], F32, name="by_s1_b", align_bytes=64, offset=BY_S1_B_AT)
         by_s2 = [sb.tile([P, V], F32, name="by_s2_%d" % t) for t in range(PACK)]
         by_d2 = [sb.tile([P, V], F32, name="by_d2_%d" % t) for t in range(PACK)]
         zb = [
@@ -186,6 +191,11 @@ def tile_picked_carry2_none_po_kernel(
         put1(D)
         fetch2(B)
         put2(B)
+        w2d = shared.tile([P, N], U32, name="w2d", align_bytes=64, offset=BY_S1_B_AT)
+        nc.scalar.copy(
+            out=w2d[:].rearrange("p (t n i) -> p n t i", t=PACK, i=4),
+            in_=w2w[:].bitcast(U32).rearrange("p (n i t) -> p n t i", t=PACK, i=4),
+        )
         fetch2(C)
         round_plane(A)
         put2(C)

@@ -18,6 +18,7 @@ COPY = mybir.ActivationFunctionType.Copy
 P = 128
 PACK = 4
 QUADRANTS = 4
+SCALE_ROWS = 16
 BANKS = 8
 BANK_COLUMNS = 256
 PIECES = (slice(0, 256), slice(256, 384), slice(384, 512))
@@ -32,6 +33,7 @@ W1_ODD_AT = W1_EVEN_AT + 2 * 2 * P * PACK
 PICKED_AT = W1_EVEN_AT
 W1_ODD_CODES_AT = 4 * N + N
 BY_S1_B_AT = W1_ODD_AT + 2 * 2 * P * PACK
+W2_WORDS_AT = BY_S1_B_AT + 4 * N
 STATES_AT, STATE_PITCH = 32 * 1024, 48 * 1024
 
 
@@ -57,23 +59,22 @@ def tile_picked_carry2_none_po_kernel(
         d2_t = lists.tile([P, V // 16], U16, name="d2_t")
 
         xs = sb.tile([P, T], U8, name="xs", align_bytes=64)
-        xs_rows = sb.tile([P, T // 4], I32, name="xs_rows", align_bytes=64)
+        xs_rows = sb.tile([SCALE_ROWS, T // 4], I32, name="xs_rows", align_bytes=64)
+        xsg = sb.tile([P, S], U8, name="xsg", align_bytes=64)
         xw = shared.tile([P, T], I32, name="xw", align_bytes=64, offset=X_WORDS_AT)
         w2s = sb.tile([P, N], U8, name="w2s", align_bytes=64)
-        w2w = sb.tile([P, N], I32, name="w2w", align_bytes=64)
         w1_raw = sb.tile([P, PACK, H], F32, name="w1_raw", align_bytes=64)
 
         nc.vector.memset(xs[:].bitcast(I32), 0)
+        nc.vector.memset(xsg[:].bitcast(I32), 0)
         nc.gpsimd.memset(w2s[:].bitcast(I32), 0)
 
-        load_scale_rows(nc.sync, xs_rows, x_scales[0], (0, 1))
-        load_scale_rows(nc.scalar, xs_rows, x_scales[0], (2, 3))
+        nc.sync.dma_start(out=xs_rows[:], in_=x_scales[0].bitcast(I32))
         nc.sync.dma_start(out=offs_t[:], in_=offs)
         nc.sync.dma_start(out=w1_raw[:], in_=w1.rearrange("(p j) c -> p j c", j=PACK))
         nc.sync.dma_start(out=xw[:], in_=x_words[0].rearrange("p c r -> p (c r)").bitcast(I32))
         load_scale_rows(nc.gpsimd, w2s[:].bitcast(I32), w2_scales[0], range(QUADRANTS))
         nc.sync.dma_start(out=s1_t[:], in_=s1)
-        nc.sync.dma_start(out=w2w[:], in_=w2_words[0].rearrange("p c r -> p (c r)").bitcast(I32))
         nc.sync.dma_start(out=d1_t[:], in_=d1)
         nc.sync.dma_start(out=s2_t[:], in_=s2)
         nc.sync.dma_start(out=d2_t[:], in_=d2)
@@ -81,11 +82,16 @@ def tile_picked_carry2_none_po_kernel(
         def entries(list_tile, part):
             return list_tile[:, part.start // 16 : part.stop // 16]
 
-        for q in range(QUADRANTS):
-            rows = slice(32 * q, 32 * q + 4)
-            nc.vector.tensor_copy(out=xs[rows, :].bitcast(I32), in_=xs_rows[rows, :])
-        xsg = sb.tile([P, S], U8, name="xsg", align_bytes=64)
-        nc.vector.tensor_copy(out=xsg[:], in_=xs[:].indirect(offs_t[:]))
+        nc.vector.tensor_copy(out=xs[0:SCALE_ROWS, :].bitcast(I32), in_=xs_rows[:])
+        picked_rows = shared.tile([P, S], U8, name="picked_rows", align_bytes=64, offset=W2_WORDS_AT)
+        nc.vector.tensor_copy(out=picked_rows[:], in_=xs[:].indirect(offs_t[:]))
+        for q in range(1, QUADRANTS):
+            nc.scalar.dma_start(
+                out=xsg[32 * q : 32 * q + 4, :].bitcast(I32), in_=picked_rows[4 * q : 4 * q + 4, :].bitcast(I32)
+            )
+        nc.vector.tensor_copy(out=xsg[0:4, :].bitcast(I32), in_=picked_rows[0:4, :].bitcast(I32))
+        w2w = shared.tile([P, N], I32, name="w2w", align_bytes=64, offset=W2_WORDS_AT)
+        nc.sync.dma_start(out=w2w[:], in_=w2_words[0].rearrange("p c r -> p (c r)").bitcast(I32))
 
         w1g = [
             shared.tile([P, 2, P, PACK], BF16, name="w1g0", align_bytes=64, offset=W1_EVEN_AT),

@@ -69,6 +69,10 @@ def tile_picked_carry2_none_po_kernel(
         nc.vector.memset(xsg[:].bitcast(I32), 0)
         nc.gpsimd.memset(w2s[:].bitcast(I32), 0)
 
+        warm = sb.tile([P, 2], F32, name="warm")
+        nc.vector.memset(warm[:, 0:1], 0.0)
+        nc.scalar.copy(out=warm[:, 1:2], in_=warm[:, 0:1])
+
         nc.sync.dma_start(out=xs_rows[:], in_=x_scales[0].bitcast(I32))
         nc.sync.dma_start(out=offs_t[:], in_=offs)
         nc.sync.dma_start(out=w1_raw[:], in_=w1.rearrange("(p j) c -> p j c", j=PACK))

@@ -176,9 +176,12 @@ def tile_picked_carry2_none_po_kernel(
         def put2(t):
             nc.vector.tensor_tensor(state[t][:].indirect(d2_t[:]), by_s2[t][:], by_d2[t][:], ADD)
 
+        def round_chunk(t, c):
+            nc.scalar.copy(out=zb[c][:, :, t], in_=state[t][:, CHUNKS[c]])
+
         def round_plane(t):
-            for c, cols in enumerate(CHUNKS):
-                nc.scalar.copy(out=zb[c][:, :, t], in_=state[t][:, cols])
+            for c in range(len(CHUNKS)):
+                round_chunk(t, c)
 
         nc.vector.tensor_copy(out=by_s1[A][:, LOWER], in_=state[A][:].indirect(entries(s1_t, LOWER)))
         fetch1(A, UPPER)
@@ -212,12 +215,14 @@ def tile_picked_carry2_none_po_kernel(
         fetch2(D)
         round_plane(B)
         put2(D)
-        round_plane(C)
+        round_chunk(C, 0)
+        round_chunk(C, 1)
 
         nc.vector.tensor_copy(out=zb[0][:, :, D], in_=state[D][:, CHUNKS[0]])
         nc.vector.tensor_copy(out=zb[1][:, 0:P, D], in_=state[D][:, CHUNKS[1].start : S // 2])
         nc.scalar.copy(out=zb[1][:, P : 2 * P, D], in_=state[D][:, S // 2 : CHUNKS[1].stop])
-        nc.scalar.copy(out=zb[2][:, :, D], in_=state[D][:, CHUNKS[2]])
+        round_chunk(C, 2)
+        round_chunk(D, 2)
 
         zq = sb.tile([P, S], U32, name="zq", align_bytes=64)
         zs = sb.tile([P, S], U8, name="zs", align_bytes=64)

from contextlib import ExitStack

import concourse.mybir as mybir

K, T, S, V, N, H = 512, 2048, 512, 256, 512, 512
FLOPS = 2 * K * H * S + 2 * H * N * S

F32 = mybir.dt.float32
BF16 = mybir.dt.bfloat16
I32 = mybir.dt.int32
U32 = mybir.dt.uint32
U16 = mybir.dt.uint16
U8 = mybir.dt.uint8
FP8X4 = mybir.dt.float8_e4m3fn_x4
ADD = mybir.AluOpType.add
COPY = mybir.ActivationFunctionType.Copy

P = 128
PACK = 4
QUADRANTS = 4
SCALE_ROWS = 16
BANKS = 8
BANK_COLUMNS = 256
PIECES = (slice(0, 256), slice(256, 384), slice(384, 512))
CHUNKS = (slice(0, 128), slice(128, 384), slice(384, 512))
A, B, C, D = 0, 2, 3, 1
WHOLE, LOWER, UPPER = slice(0, V), slice(0, V // 2), slice(V // 2, V)

X_WORDS_AT = 0
W2_SCALES_AT = 4 * N
W1_EVEN_AT = 4 * T
W1_ODD_AT = W1_EVEN_AT + 2 * 2 * P * PACK
PICKED_AT = W1_EVEN_AT
W1_ODD_CODES_AT = 4 * N + N
BY_S1_B_AT = W1_ODD_AT + 2 * 2 * P * PACK
W2_WORDS_AT = BY_S1_B_AT + 4 * N
STATES_AT, STATE_PITCH = 32 * 1024, 48 * 1024


def load_scale_rows(queue, tile, rows, quadrants):
    for q in quadrants:
        queue.dma_start(out=tile[32 * q : 32 * q + 4, :], in_=rows[4 * q : 4 * q + 4, :].bitcast(I32))


def tile_picked_carry2_none_po_kernel(
    tc, x_words, x_scales, w1, w2_words, w2_scales, offs, s1, d1, s2, d2, out_0, out_1, out_2
):
    nc = tc.nc
    with ExitStack() as ctx:
        lists = ctx.enter_context(tc.tile_pool(name="lists", bufs=1))
        sb = ctx.enter_context(tc.tile_pool(name="sb", bufs=1))
        shared = ctx.enter_context(tc.tile_pool(name="shared", bufs=1))
        psum = ctx.enter_context(tc.psum_pool(name="psum", bufs=1))

        offs_t = lists.tile([P, S // 16], U16, name="offs_t")
        s1_t = lists.tile([P, V // 16], U16, name="s1_t")
        d1_t = lists.tile([P, V // 16], U16, name="d1_t")
        s2_t = lists.tile([P, V // 16], U16, name="s2_t")
        d2_t = lists.tile([P, V // 16], U16, name="d2_t")

        xs = sb.tile([P, T], U8, name="xs", align_bytes=64)
        xs_rows = sb.tile([SCALE_ROWS, T // 4], I32, name="xs_rows", align_bytes=64)
        xsg = sb.tile([P, S], U8, name="xsg", align_bytes=64)
        xw = shared.tile([P, T], I32, name="xw", align_bytes=64, offset=X_WORDS_AT)
        w2s = sb.tile([P, N], U8, name="w2s", align_bytes=64)
        w1_raw = sb.tile([P, PACK, H], F32, name="w1_raw", align_bytes=64)

        nc.vector.memset(xs[:].bitcast(I32), 0)
        nc.vector.memset(xsg[:].bitcast(I32), 0)
        nc.gpsimd.memset(w2s[:].bitcast(I32), 0)

        warm = sb.tile([P, 2], F32, name="warm")
        nc.vector.memset(warm[:, 0:1], 0.0)
        nc.scalar.copy(out=warm[:, 1:2], in_=warm[:, 0:1])

        nc.sync.dma_start(out=xs_rows[:], in_=x_scales[0].bitcast(I32))
        nc.sync.dma_start(out=offs_t[:], in_=offs)
        nc.sync.dma_start(out=w1_raw[:], in_=w1.rearrange("(p j) c -> p j c", j=PACK))
        nc.sync.dma_start(out=xw[:], in_=x_words[0].rearrange("p c r -> p (c r)").bitcast(I32))
        load_scale_rows(nc.gpsimd, w2s[:].bitcast(I32), w2_scales[0], range(QUADRANTS))
        nc.sync.dma_start(out=s1_t[:], in_=s1)
        nc.sync.dma_start(out=d1_t[:], in_=d1)
        nc.sync.dma_start(out=s2_t[:], in_=s2)
        nc.sync.dma_start(out=d2_t[:], in_=d2)

        def entries(list_tile, part):
            return list_tile[:, part.start // 16 : part.stop // 16]

        nc.vector.tensor_copy(out=xs[0:SCALE_ROWS, :].bitcast(I32), in_=xs_rows[:])
        picked_rows = shared.tile([P, S], U8, name="picked_rows", align_bytes=64, offset=W2_WORDS_AT)
        nc.vector.tensor_copy(out=picked_rows[:], in_=xs[:].indirect(offs_t[:]))
        for q in range(1, QUADRANTS):
            nc.scalar.dma_start(
                out=xsg[32 * q : 32 * q + 4, :].bitcast(I32), in_=picked_rows[4 * q : 4 * q + 4, :].bitcast(I32)
            )
        nc.vector.tensor_copy(out=xsg[0:4, :].bitcast(I32), in_=picked_rows[0:4, :].bitcast(I32))
        w2w = shared.tile([P, N], I32, name="w2w", align_bytes=64, offset=W2_WORDS_AT)
        nc.sync.dma_start(out=w2w[:], in_=w2_words[0].rearrange("p c r -> p (c r)").bitcast(I32))

        w1g = [
            shared.tile([P, 2, P, PACK], BF16, name="w1g0", align_bytes=64, offset=W1_EVEN_AT),
            shared.tile([P, 2, P, PACK], BF16, name="w1g1", align_bytes=64, offset=W1_ODD_AT),
        ]
        raw = w1_raw[:].rearrange("p j (m a b) -> p b m j a", a=2, b=2)
        nc.vector.tensor_copy(out=w1g[0][:].rearrange("p a m j -> p m j a"), in_=raw[:, 0])
        nc.scalar.copy(out=w1g[1][:].rearrange("p a m j -> p m j a"), in_=raw[:, 1])
        w1q = [
            sb.tile([P, H // 2], U32, name="w1q0", align_bytes=64),
            shared.tile([P, H // 2], U32, name="w1q1", align_bytes=64, offset=W1_ODD_CODES_AT),
        ]
        w1s = [sb.tile([P, H // 2], U8, name="w1s%d" % b, align_bytes=64) for b in range(2)]

        def quantise_w1(b):
            nc.vector.quantize_mx(
                out=w1q[b][:].bitcast(FP8X4), scales=w1s[b][:], in_=w1g[b][:].rearrange("p a m j -> p (a m j)")
            )

        quantise_w1(0)

        xg = shared.tile([P, S], U32, name="xg", align_bytes=64, offset=PICKED_AT)
        for cols in PIECES:
            nc.vector.tensor_copy(out=xg[:, cols], in_=xw[:].bitcast(U32).indirect(entries(offs_t, cols)))

        quantise_w1(1)
        w2sd = shared.tile([P, PACK, P], U8, name="w2sd", align_bytes=64, offset=W2_SCALES_AT)
        nc.vector.tensor_copy(out=w2sd[:], in_=w2s[:].rearrange("p (m t) -> p t m", t=PACK))

        state = [
            shared.tile([P, S], F32, name="state%d" % t, align_bytes=64, offset=STATES_AT + t * STATE_PITCH)
            for t in range(PACK)
        ]

        def project(bank, t, cols):
            m_cols = slice(t // 2 * P, (t // 2 + 1) * P)
            acc = psum.tile([P, cols.stop - cols.start], F32, name="y_acc", tag="bank%d" % bank)
            nc.tensor.matmul_mx(
                out=acc[:],
                lhsT=w1q[t % 2][:, m_cols].bitcast(FP8X4),
                lhsT_scale=w1s[t % 2][:, m_cols],
                rhs=xg[:, cols].bitcast(FP8X4),
                rhs_scale=xsg[:, cols],
                start=True,
                stop=True,
            )
            return acc

        for bank, cols in enumerate(PIECES):
            nc.scalar.copy(out=state[A][:, cols], in_=project(bank, A, cols)[:])
        left, right = slice(0, S // 2), slice(S // 2, S)
        nc.vector.tensor_copy(out=state[B][:, left], in_=project(len(PIECES), B, left)[:])

        by_s1 = {t: sb.tile([P, V], F32, name="by_s1_%d" % t) for t in (A, C, D)}
        by_s1[B] = shared.tile([P, V], F32, name="by_s1_b", align_bytes=64, offset=BY_S1_B_AT)
        by_s2 = [sb.tile([P, V], F32, name="by_s2_%d" % t) for t in range(PACK)]
        by_d2 = [sb.tile([P, V], F32, name="by_d2_%d" % t) for t in range(PACK)]
        zb = [
            sb.tile([P, cols.stop - cols.start, PACK], BF16, name="zb%d" % c, align_bytes=64)
            for c, cols in enumerate(CHUNKS)
        ]

        y_acc = {}

        def empty(t, cols):
            nc.scalar.copy(out=state[t][:, cols], in_=y_acc[t][:, cols])

        def fetch1(t, part):
            nc.scalar.activation(by_s1[t][:, part], state[t][:].indirect(entries(s1_t, part)), COPY)

        def put1(t):
            nc.vector.tensor_copy(out=state[t][:].indirect(d1_t[:]), in_=by_s1[t][:])

        def fetch2(t):
            nc.scalar.activation(by_s2[t][:], state[t][:].indirect(s2_t[:]), COPY, scale=0.5)
            nc.scalar.activation(by_d2[t][:], state[t][:].indirect(d2_t[:]), COPY, scale=0.5)

        def put2(t):
            nc.vector.tensor_tensor(state[t][:].indirect(d2_t[:]), by_s2[t][:], by_d2[t][:], ADD)

        def round_chunk(t, c):
            nc.scalar.copy(out=zb[c][:, :, t], in_=state[t][:, CHUNKS[c]])

        def round_plane(t):
            for c in range(len(CHUNKS)):
                round_chunk(t, c)

        nc.vector.tensor_copy(out=by_s1[A][:, LOWER], in_=state[A][:].indirect(entries(s1_t, LOWER)))
        fetch1(A, UPPER)
        put1(A)
        b_right = project(0, B, right)
        y_acc[C] = project(1, C, slice(0, S))
        nc.scalar.copy(out=state[B][:, right], in_=b_right[:])
        y_acc[D] = project(0, D, slice(0, S))
        empty(C, left)
        fetch1(B, WHOLE)
        put1(B)
        empty(C, right)
        empty(D, left)
        fetch1(C, WHOLE)
        put1(C)
        empty(D, right)
        fetch2(A)
        put2(A)
        fetch1(D, WHOLE)
        put1(D)
        fetch2(B)
        put2(B)
        w2d = shared.tile([P, N], U32, name="w2d", align_bytes=64, offset=BY_S1_B_AT)
        nc.scalar.copy(
            out=w2d[:].rearrange("p (t n i) -> p n t i", t=PACK, i=4),
            in_=w2w[:].bitcast(U32).rearrange("p (n i t) -> p n t i", t=PACK, i=4),
        )
        fetch2(C)
        round_plane(A)
        put2(C)
        fetch2(D)
        round_plane(B)
        put2(D)
        round_chunk(C, 0)
        round_chunk(C, 1)

        nc.vector.tensor_copy(out=zb[0][:, :, D], in_=state[D][:, CHUNKS[0]])
        nc.vector.tensor_copy(out=zb[1][:, 0:P, D], in_=state[D][:, CHUNKS[1].start : S // 2])
        nc.scalar.copy(out=zb[1][:, P : 2 * P, D], in_=state[D][:, S // 2 : CHUNKS[1].stop])
        round_chunk(C, 2)
        round_chunk(D, 2)

        zq = sb.tile([P, S], U32, name="zq", align_bytes=64)
        zs = sb.tile([P, S], U8, name="zs", align_bytes=64)
        oq = sb.tile([P, S], U32, name="oq", align_bytes=64)
        osc = sb.tile([P, S], U8, name="osc", align_bytes=64)
        out_rows = out_0.rearrange("(p t) j -> p t j", t=PACK)
        out_words = out_1[0].rearrange("p c r -> p (c r)").bitcast(I32)

        for c, cols in enumerate(CHUNKS):
            nc.vector.quantize_mx(
                out=zq[:, cols].bitcast(FP8X4), scales=zs[:, cols], in_=zb[c][:].rearrange("p n t -> p (n t)")
            )

        bank = BANKS - 1
        results = []
        for c, cols in enumerate(CHUNKS):
            width = cols.stop - cols.start
            is_last_chunk = c == len(CHUNKS) - 1
            o32 = sb.tile([P, PACK, width], F32, name="o32_%d" % c)
            results.append(o32)
            per_bank = BANK_COLUMNS // width
            for t0 in range(0, PACK, per_bank):
                planes = slice(t0, t0 + per_bank)
                acc = psum.tile([P, per_bank, width], F32, name="o_acc", tag="bank%d" % (bank % BANKS))
                bank = bank + 1
                for t in range(planes.start, planes.stop):
                    m_cols = slice(t * P, (t + 1) * P)
                    nc.tensor.matmul_mx(
                        out=acc[:, t - t0, :],
                        lhsT=w2d[:, m_cols].bitcast(FP8X4),
                        lhsT_scale=w2sd[:, t, :],
                        rhs=zq[:, cols].bitcast(FP8X4),
                        rhs_scale=zs[:, cols],
                        start=True,
                        stop=True,
                    )
                nc.scalar.copy(out=o32[:, planes, :], in_=acc[:])
                if not is_last_chunk and planes.stop % 2 == 0:
                    pair = slice(planes.stop - 2, planes.stop)
                    nc.sync.dma_start(out=out_rows[:, pair, cols], in_=o32[:, pair, :])
            if is_last_chunk:
                nc.sync.dma_start(out=out_rows[:, :, cols], in_=o32[:])

        for c, (cols, o32) in enumerate(zip(CHUNKS, results)):
            width = cols.stop - cols.start
            is_last_chunk = c == len(CHUNKS) - 1
            ob = sb.tile([P, width, PACK], BF16, name="ob%d" % c, align_bytes=64)
            nc.vector.tensor_copy(
                out=ob[:].rearrange("p (n i) t -> p n t i", i=4), in_=o32[:].rearrange("p t (n i) -> p n t i", i=4)
            )
            nc.vector.quantize_mx(
                out=oq[:, cols].bitcast(FP8X4), scales=osc[:, cols], in_=ob[:].rearrange("p n t -> p (n t)")
            )
            if c > 0:
                done = cols if is_last_chunk else slice(0, cols.stop)
                nc.scalar.dma_start(out=out_words[:, done], in_=oq[:, done].bitcast(I32))
        for q in range(QUADRANTS):
            nc.sync.dma_start(
                out=out_2[0, 4 * q : 4 * q + 4, :].bitcast(I32), in_=osc[32 * q : 32 * q + 4, :].bitcast(I32)
            )
